import numpy as np, ml_dtypes
CORES = [8,136,40,168]
N = 4
BF = ml_dtypes.bfloat16
def gentries(a):
    return np.ascontiguousarray(a.reshape(8, 16, -1).transpose(0, 2, 1)).reshape(8, -1)
def gtable(e):
    e = np.asarray(e); return np.ascontiguousarray(e.reshape(8, -1, 16).transpose(0, 2, 1)).reshape(128, -1).astype(np.int32)
V, E, LB, ST, RO = 3072, 1024, 10, 4, 3
def parts(rng):
    Q = 8 * N; q = np.arange(Q)[:, None]; k = np.arange(V)[None, :]
    o = np.argsort(rng.random((Q, V)), axis=1)
    x = np.zeros((Q, V, 16), np.float32); x[q, o] = np.linspace(235.0, 20.0, V)[None, :, None]
    x = x + rng.integers(4, 48, (Q, 1, 1)).astype(np.float32) * rng.standard_normal((Q, V, 16), dtype=np.float32)
    x = np.clip(np.floor(x), 0, 255)
    top = rng.integers(40, 700, (Q, 1)); nx = k + rng.integers(1, top + 1, (Q, V))
    nx = np.where((nx >= V) | (rng.random((Q, V)) < 0.015625), k, nx)
    S = np.zeros((Q, V), np.int64); S[q, o] = o[q, nx]
    pa = rng.integers(0, V, (Q, E)); far = np.where(rng.random((Q, E)) < 0.5, rng.integers(1, V, (Q, E)), rng.integers(1, 301, (Q, E)))
    a = o[q, pa]; b = o[q, (pa + far) % V]
    sa = S[q, a]; b = np.where((rng.random((Q, E)) < 0.0625) & (sa != a), sa, b)
    ix = np.where(rng.random((Q, E)) < 0.0625, rng.integers(0, E, (Q, E)), np.arange(E)[None, :])
    return x, S, a[q, ix], b[q, ix]
def pack(x, S, a, b):
    return {"x": np.ascontiguousarray(np.asarray(x).reshape(N, 8, V, 16).transpose(0, 1, 3, 2)).reshape(N, 128, V).astype(np.float32).astype(BF),
            "succ": np.ascontiguousarray(S.reshape(N, 8, V)).astype(np.int32),
            "ea": np.stack([gtable(e) for e in a.reshape(N, 8, E)]), "eb": np.stack([gtable(e) for e in b.reshape(N, 8, E)])}
def setup_inputs(rng):
    return pack(*parts(rng))
def setup_inputs_ties(rng):
    x, S, a, b = parts(rng); Q = 8 * N
    D = np.zeros((5, 16), np.int64); D[1, :8] = 1; D[1, 8:] = -1; D[2, :9] = 1; D[2, 9:] = -1; D[3, 0] = 1; D[4, 15] = -1
    A = rng.integers(1, 255, (Q, 1, 16)); A[3::8] = rng.choice(np.array([0, 255]), (N, 1, 16))
    y = np.clip(A + D[rng.integers(0, 5, (Q, V))], 0, 255)
    y[5::8] = A[5::8]; y[7::8] = x[7::8].astype(np.int64)
    for i in range(6, Q, 8):
        S[i] = np.where(S[i] % (V - 1) == 0, np.arange(V), S[i]); S[i, 0] = 0; S[i, V - 1] = V - 1
        hit = (a[i] % (V - 1) == 0) | (b[i] % (V - 1) == 0)
        a[i] = np.where(hit, 1, a[i]); b[i] = np.where(hit, 2, b[i])
        j = int(rng.integers(0, E)); a[i, j] = 0; b[i, j] = V - 1
        y[i, 0] = np.minimum(y[i, 0], 200); y[i, V - 1] = y[i, 0]; y[i, V - 1, int(rng.integers(0, 16))] += 50
    return pack(y, S, a, b)
def setup_inputs_crowd(rng):
    x, S, a, b = parts(rng); k = np.arange(E); v = np.arange(V)
    used = np.array(sorted({(ST * n + j) % LB for n in range(RO) for j in range(1, ST)}))
    hub = rng.permutation(V)
    for i in range(8 * N):
        g = i % 8; p = rng.permutation(V)
        if g in (0, 2, 4):
            d = (1, ST + 1, int(rng.choice(used)))[g // 2]; m = k & ~(1 << d)
            a[i] = p[2 * m]; b[i] = p[2 * m + 1]; S[i] = v
        elif g == 1:
            y = rng.permutation(E); j = np.arange(E - 257)
            a[i, y[:257]] = hub[0]; b[i, y[:257]] = hub[1]
            a[i, y[257:]] = hub[2 + 2 * j]; b[i, y[257:]] = hub[3 + 2 * j]
            S[i] = v; x[i] = np.minimum(x[i], 254); x[i, hub[0]] = 255
        elif g == 3:
            a[i] = p[rng.integers(0, 8, E)]; b[i] = p[8 + rng.integers(0, V - 8, E)]; x[i, p[:8]] = 255
        elif g == 5 and i // 8 == N - 1:
            a[i] = p[2 * k]; b[i] = p[2 * k + 1]; S[i] = v
        elif g == 5:
            n = V // 8
            if (i // 8) % 2 == 0: H = int(rng.integers(0, V - n + 1)) + np.arange(n)
            else: H = 8 * np.arange(n) + int(rng.integers(0, 8))
            z = rng.permutation(np.setdiff1d(v, H)); y = rng.permutation(E); j = np.arange(E - n)
            w = np.concatenate([z[:(ST - 1) * n].reshape(ST - 1, n), rng.permutation(H)[None, :]]); z = z[(ST - 1) * n:]
            S[i] = v; S[i, w[:-1]] = w[1:]
            x[i] = rng.integers(0, 128, (V, 16)); x[i, w] += 128
            a[i, y[:n]] = w[0]; b[i, y[:n]] = rng.permutation(z)[:n]
            a[i, y[n:]] = z[2 * j]; b[i, y[n:]] = z[2 * j + 1]
        elif g == 6:
            y = rng.permutation(k[((k >> 1) & 1) == 0]); c = np.concatenate([k[((k >> 1) & 1) == 1], y[:1]]); j = np.arange(E // 2 - 1)
            a[i, c] = hub[0]; b[i, c] = hub[1 + rng.permutation(E // 2 + 1)]
            a[i, y[1:]] = hub[E + 2 * j]; b[i, y[1:]] = hub[E + 2 * j + 1]
            S[i] = v; x[i] = np.minimum(x[i], 254); x[i, hub[0]] = 255
        else:
            m = np.where(((k >> 1) & 1) == 1, k & ~8, k)
            a[i] = p[2 * m]; b[i] = p[2 * m + 1]; S[i] = v
    return pack(x, S, a, b)
def setup_inputs_chains(rng):
    Q = 8 * N; q = np.arange(Q)[:, None]; k = np.arange(V)[None, :]
    C = rng.choice(np.array([2, 3, 4, 8, 16]), (Q, 1)); o = np.argsort(rng.random((Q, V)), axis=1)
    nx = k + C; nx = np.where(nx >= V, k, nx)
    S = np.zeros((Q, V), np.int64); S[q, o] = o[q, nx]
    x = np.zeros((Q, V, 16)); x[q, o] = np.floor(np.linspace(250.0, 1.0, V)[None, :, None] + 0.0625 * np.arange(16)[None, None, :])
    pa = rng.integers(0, V - 32, (Q, E)); pb = pa + rng.integers(1, C, (Q, E)); turn = rng.random((Q, E)) < 0.5
    return pack(x, S, o[q, np.where(turn, pb, pa)], o[q, np.where(turn, pa, pb)])
def setup_inputs_ends(rng):
    x, S, a, b = parts(rng); v = np.arange(V)
    x[0::2] = rng.choice(np.array([0.0, 255.0]), (4 * N, V, 16))
    S[0::8] = rng.integers(0, V, (N, V)); S[1::8] = 0; S[2::8] = V - 1; S[3::8] = V - 1 - v; S[4::8] = (v + 1) % V
    S[5::8] = v ^ 1; b[5::8] = a[5::8] ^ 1
    x[5::16] = rng.integers(0, 64, (N // 2, V, 16)) + 64 * (3 - v % 4)[None, :, None]
    S[5::16] = v - v % 4 + (v + 1) % 4; a[5::16] = 4 * rng.integers(0, V // 4, (N // 2, E)); b[5::16] = a[5::16] + 2
    w = 2 + rng.permutation(V - 4); M = V - 4 - 2 * ST
    for i in range(6, 8 * N, 8):
        S[i] = v; S[i, w[2 * ST:]] = rng.choice(w[2 * ST:], M)
        u = rng.integers(0, M, E); a[i] = w[2 * ST + u]; b[i] = w[2 * ST + (u + rng.integers(1, M, E)) % M]
        for c, (e, low) in enumerate(((0, 1), (V - 1, V - 2))):
            way = np.append(w[c * ST:(c + 1) * ST], e)
            S[i, way[:-1]] = way[1:]; x[i, way] = 255; x[i, low] = 0
        j = rng.permutation(E)[:2]
        a[i, j] = np.array([w[0], V - 2]); b[i, j] = np.array([1, w[ST]])
    a[7::8] = V - 1; b[7::8] = rng.integers(0, V - 1, (N, E))
    return pack(x, S, a, b)
def setup_inputs_spread(rng):
    Q = 8 * N
    x = np.minimum(np.floor(np.exp2(8 * rng.random((Q, V, 1))) * rng.random((Q, V, 16))), 255)
    S = rng.integers(0, V, (Q, V)); S = np.where(rng.random((Q, V)) < 0.0625, np.arange(V)[None, :], S)
    a = rng.integers(0, V, (Q, E)); b = (a + rng.integers(1, V, (Q, E))) % V
    return pack(x, S, a, b)
def check_inputs(d):
    bad = []; v = np.asarray(d["x"]).astype(np.float32)
    if not np.all((v >= 0) & (v <= 255) & (v == np.floor(v))): bad.append("x")
    for k in ("succ", "ea", "eb"):
        if np.min(d[k]) < 0 or np.max(d[k]) > V - 1: bad.append("range of " + k)
    if np.any(np.asarray(d["ea"]) == np.asarray(d["eb"])): bad.append("an edge with equal ends")
    return bad
def above(X, a, b):
    q = np.arange(X.shape[0])[:, None]
    m = np.add.reduce(np.sign(X[q, a] - X[q, b]), axis=2)
    return (m > 0) | ((m == 0) & (a < b))
def reference(x, succ, ea, eb):
    Q = 8 * N; q = np.arange(Q)[:, None]; lane = np.arange(E)[None, :]; qq = np.broadcast_to(q, (Q, E))
    X = np.ascontiguousarray(x.astype(np.float32).astype(np.int32).reshape(Q, 16, V).transpose(0, 2, 1))
    S = np.array(succ, np.int64).reshape(Q, V)
    fa = np.concatenate([gentries(e) for e in ea]).astype(np.int64); fb = np.concatenate([gentries(e) for e in eb]).astype(np.int64)
    a, b = fa, fb
    for rnd in range(RO):
        up = above(X, a, b); h = np.where(up, a, b); l = np.where(up, b, a)
        done = np.zeros((Q, E), bool); out = np.zeros((Q, E), bool)
        for k in range(ST):
            act = ~done & ~out
            s = S[q, h]
            met = act & (s == l)
            walk = act & ~met & (s != h) & above(X, s, l)
            ask = act & ~met & ~walk
            place = q * V + h
            n = np.bincount(place[ask], minlength=Q * V)[place]
            sole = ask & (n == 1); into = sole & (s != h)
            S[qq[sole], h[sole]] = l[sole]
            done = done | met | (sole & (s == h))
            h, l = np.where(into, l, np.where(walk, s, h)), np.where(into, s, l)
            out = ask & (n > 1) & (((lane >> ((rnd * ST + k + 1) % LB)) & 1) == 1)
        X = X + np.clip(X[q, S] - X, -1, 1)
        a = np.roll(np.where(done, fa, h), 8, axis=0); b = np.roll(np.where(done, fb, l), 8, axis=0)
        fa = np.roll(fa, 8, axis=0); fb = np.roll(fb, 8, axis=0)
    return {"ys": S.reshape(N, 8, V).astype(np.float32), "yx": np.ascontiguousarray(X.transpose(0, 2, 1)).reshape(N, 128, V).astype(np.float32).astype(BF)}

@@ -1,0 +1,456 @@
+from concourse.mybir import AluOpType as A, ActivationFunctionType as F
+
+RO, ST, LB = 3, 4, 10
+BIG = 131072.0
+BS, GP, EC = 36, 48, 5
+NV = 56
+NW = 128 - 2 * NV
+N1, N2, M1, M2 = 7, 8, 4, 4
+DT = {"b": "bfloat16", "f": "float32", "i": "int32", "u": "uint16"}
+SCRATCH = {"BB": ("sbuf", [128, 128 * NV], "bfloat16"), "BT": ("sbuf", [128, 130 * (64 - NV)], "bfloat16"),
+           "AN": ("sbuf", [128, 8 * NW], "bfloat16")}
+for _t in ("b3072 XA XB CT;b4096 SW;b3088 OH;b1024 GE GS XL LD SG AR AT GF;b1536 DD XS SN XP XM;"
+           "b64 LW;f64 NL;b128 FL0 FL1 BD IO IDP IDN IDE IDL IDF;b130 IOX;b256 FT WR;i128 C1 FI EI;f128 C0 I32P I32N EF PF2;"
+           "b2048 SELS SELM SELF;b8 SL2;i1 PI GI QI;f1 PF GFC QF GC WS WT WF WH;f16 EQ EQW;i192 UI VI W1 W2 W3 V1 V2 SI;"
+           "b192 D0 D1 D2 S0 S1;f192 Y2 Y3;u192 SL16;i64 LI LN H OI;i640 BI;b640 BITS;u128 ED EDN LP0 LP1 SP0 SP1;"
+           "f64 TR L D SH N3 HX WK T1 H1 LH AK AB SC SO SE T2 T3 NS UP;u64 H16 L16 S16 OF16 HX16 SC16;"
+           "b64 EH EL NM NA DN SD SIT").split(";"):
+    for _n in _t.split()[1:]:
+        SCRATCH[_n] = ("sbuf", [128, int(_t.split()[0][1:])], DT[_t[0]])
+for _n in ("pS", "pV", "pX", "pL", "pH"):
+    SCRATCH[_n] = ("psum", [128, 512], "float32")
+for _n in ("pT0", "pT1", "pF"):
+    SCRATCH[_n] = ("psum", [128, 1024], "bfloat16")
+PS = ("pS", "pV", "pX", "pL", "pH", "pT0", "pT1", "pF")
+SEMAPHORES = ["cv", "ca", "cp", "cg", "se", "s0", "s1", "re", "r0", "r1"] + ["d%d" % i for i in range(24)]
+CT = "CT CT0 CT1 CT2"
+SW = "SW SWh SWl"
+
+
+def rank_program(g, core, T, topo):
+    rank = T.rank_of(core)
+    if rank is None:
+        return
+    N = len(T.cores)
+    nxt, prv = T.cores[(rank + 1) % N], T.cores[(rank - 1) % N]
+    eng = {"v": g.vector, "a": g.scalar, "p": g.tensor, "g": g, "s": g.sync}
+    total, seen, wr_, rd_ = {}, {e: {} for e in eng}, {}, {}
+
+    def need(e, toks):
+        best = {}
+        for t in toks:
+            if t[0] not in best or best[t[0]][1] < t[1]:
+                best[t[0]] = t
+        for t in sorted(best.values(), key=lambda t: -len(t[3])):
+            if seen[e].get(t[0], 0) < t[1]:
+                eng[e].wait_ge(T.sem[t[0]], t[1])
+                seen[e][t[0]] = t[1]
+                for s, v in t[3].items():
+                    seen[e][s] = max(seen[e].get(s, 0), v)
+
+    def before(e, rd, wr):
+        toks = []
+        for k in rd:
+            toks += wr_.get(k, {}).values()
+            if k in PS:
+                toks += [t for t in rd_.get(k, {}).values() if t[2] != e]
+        for k in wr:
+            part = k[0] == "+" or (e == "p" and k in PS)
+            k = k.strip("+")
+            toks += [t for t in wr_.get(k, {}).values() if not (part and t[2] == e)]
+            toks += rd_.get(k, {}).values()
+        need(e, toks)
+
+    def after(tok, rd, wr):
+        for k in wr:
+            part = k[0] == "+"
+            k = k.strip("+")
+            if not part:
+                wr_[k] = {}
+            wr_.setdefault(k, {})[tok[0]] = tok
+            rd_[k] = {}
+        for k in rd:
+            if k not in wr:
+                rd_.setdefault(k, {})[tok[0]] = tok
+
+    def em(e, fn, rd, wr):
+        rd, wr = rd.split(), wr.split()
+        before(e, rd, wr)
+        s = "c" + e
+        total[s] = total.get(s, 0) + 1
+        fn().then_inc(T.sem[s], 1)
+        after((s, total[s], e, dict(seen[e])), rd, wr)
+
+    nd = [0]
+
+    def dma(e, out, in_, rd, wr):
+        rd, wr = rd.split(), wr.split()
+        before(e, rd, wr)
+        s = "d%d" % nd[0]
+        nd[0] += 1
+        total[s] = 16
+        eng[e].dma_start(out, in_).then_inc(T.sem[s], 16)
+        after((s, 16, "D", dict(seen[e])), rd, wr)
+
+    def send(out, in_, rs, ls, rd):
+        before("g", rd.split(), [])
+        rid, pid = topo.addr(nxt, core)
+        g.remote_dma(out, in_, T.sem[rs], T.sem[ls], pid, rid, topo.mask(core, nxt))
+        total[ls] = len(topo.engines(core, nxt))
+        total[rs] = len(topo.engines(prv, core))
+        after((ls, total[ls], "D", {}), rd.split(), [])
+
+    def landed(rs, key):
+        wr_[key] = {rs: (rs, total[rs], "N", {})}
+
+    def cp(out, in_, rd, wr):
+        em("v", lambda: g.vector.tensor_copy(out, in_), rd, wr)
+
+    def tt(out, a, b, op, rd, wr):
+        em("v", lambda: g.vector.tensor_tensor(out, a, b, op), rd, wr)
+
+    def ts(out, a, s1, op0, rd, wr, s2=None, op1=None):
+        if op1 is None:
+            em("v", lambda: g.vector.tensor_scalar(out, a, s1, None, op0), rd, wr)
+        else:
+            em("v", lambda: g.vector.tensor_scalar(out, a, s1, s2, op0, op1), rd, wr)
+
+    def ms(ap, c, wr):
+        em("v", lambda: g.vector.memset(ap, c), "", wr)
+
+    def act(out, in_, fn, rd, wr, bias=0.0, scale=1.0):
+        em("a", lambda: g.scalar.activation(out, in_, fn, bias=bias, scale=scale), rd, wr)
+
+    def mm(out, l, r, start, stop, rd, wr):
+        em("p", lambda: g.tensor.matmul(out, l, r, start, stop), rd, wr)
+
+    def tr(out, in_, rd, wr):
+        em("p", lambda: g.tensor.transpose(out, in_, T.IDP[:]), rd + " IDP", wr)
+
+    def gat(e, out, win, off, rd, wr):
+        if e == "v":
+            cp(out, win.indirect(off), rd, wr)
+        else:
+            act(out, win.indirect(off), F.Copy, rd, wr)
+
+    def ext(ps, key, sel, selkey, src, rd, start, n=64, o=0):
+        for q in range(16):
+            mm(ps[:, 0:n], sel[:, q * 128:(q + 1) * 128], src[:, 16 * o + q:16 * (o + n):16], start and q == 0, q == 15,
+               rd + " " + selkey, key)
+
+    dma("s", T.EI[:, 0:64], T.ea[:], "", "EIa")
+    dma("a", T.EI[:, 64:128], T.eb[:], "", "EIb")
+    dma("a", T.SI[:], T.succ[:], "", "SI")
+    dma("s", T.XA[:], T.x[:], "", "X0a X0b")
+
+    def iota(ap, pat, base, cm, wr, **kw):
+        em("g", lambda: g.iota(ap, pat, base, cm, **kw), "", wr)
+    iota(T.PI[:], [[1, 1]], 0, 1, "PI")
+    iota(T.FI[:], [[1, 128]], 0, 0, "FI")
+    iota(T.UI[:], [[1, 192]], 0, 192, "UI")
+    iota(T.LI[:], [[16, 64]], 0, 0, "LI")
+    iota(T.IOX[:], [[1, 130]], -1, 0, "IOX", allow_small_or_imprecise_dtypes=True)
+    ms(T.SELM[:], 0.0, "SELM")
+    ts(T.GI[:], T.PI[:], 4, A.arith_shift_right, "PI", "GI")
+    ts(T.QI[:], T.PI[:], 15, A.bitwise_and, "PI", "QI")
+    cp(T.PF[:], T.PI[:], "PI", "PF")
+    ts(T.C1[:], T.FI[:], 4, A.arith_shift_right, "FI", "C1")
+    cp(T.GFC[:], T.GI[:], "GI", "GFC")
+    cp(T.QF[:], T.QI[:], "QI", "QF")
+    cp(T.IO[:], T.FI[:], "FI", "IO")
+    ts(T.BD[:], T.C1[:], T.GFC[:], A.is_equal, "C1 GFC", "BD", 4096.0, A.mult)
+    ts(T.EQ[:], T.FI[:, 0:16], T.QF[:], A.is_equal, "FI QF", "EQ")
+    ts(T.GC[:], T.GFC[:], -3072.0, A.mult, "GFC", "GC")
+    ms(T.SW[:], 0.0, SW)
+    ts(T.WF[:], T.QF[:], 11.5, A.is_lt, "QF", "WF", -BIG / 4096, A.mult)
+    ts(T.VI[:], T.UI[:], T.GC[:], A.add, "UI GC", "VI")
+    ts(T.WS[:], T.EQ[:, 0:1], 64.0 / 4096, A.mult, "EQ", "WS")
+    for q in range(16):
+        cp(T.SELM[:, q * 128 + q:(q + 1) * 128:16], T.BD[:, 0:128:16], "BD", "SELM" if q == 0 else "+SELM")
+    ts(T.WT[:], T.EQ[:, 1:2], 1.0 / 4096, A.mult, "EQ WS", "WT", T.WS[:], A.add)
+    cp(T.ED[:], T.EI[:], "EIa EIb", "ED")
+    send(T.EDN[:], T.ED[:], "re", "se", "ED")
+    ts(T.W1[:], T.SI[:], 6, A.arith_shift_right, "SI", "W1")
+    ts(T.W2[:], T.SI[:], 63, A.bitwise_and, "SI", "W2")
+    cp(T.S0[:], T.W1[:], "W1", "S0")
+    cp(T.S1[:], T.W2[:], "W2", "S1")
+    act(T.SELS[:], T.SELM[:], F.Identity, "SELM WT", "SELS", scale=T.WT[:])
+    dma("s", T.SW[0:128:16, 0:3072], T.S0[:], "S0", "SWh")
+    dma("s", T.SW[1:128:16, 0:3072], T.S1[:], "S1", "SWl")
+    ms(T.CT[:], 0.0, CT)
+    ts(T.V1[:], T.VI[:], 6, A.arith_shift_right, "VI", "V1")
+    ts(T.V2[:], T.VI[:], 63, A.bitwise_and, "VI", "V2")
+    ts(T.W3[:], T.VI[:], 127, A.bitwise_and, "VI", "W3")
+    cp(T.D2[:], T.W3[:], "W3", "D2")
+    cp(T.D0[:], T.V1[:], "V1", "D0")
+    cp(T.D1[:], T.V2[:], "V2", "D1")
+    for k in (2, 0, 1):
+        dma("s", T.CT[k:128:16, :], T["D%d" % k][:], "D%d" % k, "CT%d" % k)
+    for nm, sc in (("IDN", -1.0), ("IDP", 1.0), ("I32N", -1.0)):
+        ts(T[nm][:], T.FI[:], T.PF[:], A.is_equal, "FI PF", nm, sc, A.mult)
+    ts(T.SL2[:], T.BD[:, 0:128:16], T.EQ[:, 2:3], A.mult, "BD EQ", "SL2", 1.0 / 4096, A.mult)
+
+    def late_constants():
+        for nm, sc in (("IDE", -BIG / 4096), ("IDL", 4 * BIG / 4096), ("IDF", 4096.0), ("I32P", 1.0)):
+            ts(T[nm][:], T.FI[:], T.PF[:], A.is_equal, "FI PF", nm, sc, A.mult)
+        ms(T.WR[:, 0:128], 1.0, "+WR")
+        ms(T.WR[:, 128:256], 2048.0, "+WR")
+        ms(T.OH[:, 3072:3088], 0.0, "+OH")
+        ts(T.WH[:], T.PF[:], 2.0 * NV - 0.5, A.is_gt, "PF", "WH", -0.5, A.mult)
+        ts(T.LN[:], T.LI[:], T.QF[:], A.add, "LI QF", "LN")
+        ts(T.EQW[:], T.EQ[:], T.WH[:], A.mult, "EQ WH", "EQW")
+        ts(T.TR[:], T.LN[:], 3072.0, A.add, "LN", "TR")
+        tt(T.EQW[:], T.EQ[:], T.EQW[:], A.add, "EQ EQW", "EQW")
+        for k in range(12):
+            ts(T.OH[:, 256 * k:256 * k + 256], T.WR[:], T.EQW[:, k:k + 1], A.mult, "WR EQW", "+OH")
+        zs = sorted({(ST * n + k) % LB for n in range(RO) for k in range(1, ST)})
+        for z in zs:
+            ts(T.BI[:, 64 * z:64 * z + 64], T.LN[:], z, A.arith_shift_right, "LN", "BI%d" % z, 1, A.bitwise_and)
+        for z in zs:
+            ts(T.BITS[:, 64 * z:64 * z + 64], T.BI[:, 64 * z:64 * z + 64], 4096.0, A.mult, "BI%d" % z, "BITS%d" % z)
+
+    def signs(X, xk, lst, lk):
+        m = 16 * BS
+        tt(T.DD[:, 0:m], X[:].indirect(lst[:, 0:BS]), T.XL[:, 0:m], A.subtract, xk + " XL0 XL1 " + lk, "DD")
+        gat("a", T.XS[:, 0:1024 - m], X[:], lst[:, BS:64], xk + " " + lk, "XS0")
+        mm(T.pH[:, 0:1024 - m], T.IDN[:], T.XL[:, m:1024], True, False, "IDN XL0 XL1", "pH")
+        mm(T.pH[:, 0:1024 - m], T.IDP[:], T.XS[:, 0:1024 - m], False, True, "IDP XS0", "pH")
+        act(T.SG[:, m:1024], T.pH[:, 0:1024 - m], F.Sign, "pH", "SG1")
+
+    def clip():
+        ts(T.SG[:, 0:16 * BS], T.DD[:, 0:16 * BS], 1.0, A.min, "DD", "SG0", -1.0, A.max)
+
+    def digits(X, xk, first):
+        if first:
+            gat("a", T.XL[:], X[:], T.L16[:], xk + " L16", "XL0 XL1")
+        gat("a", T.GE[:], T.CT[:], T.H16[:], CT + " H16", "GE")
+        for c in range(8):
+            mm(T.pL[:, 8 * c:8 * c + 8], T.GE[:, 128 * c:128 * c + 128], T.SL2[:], True, True, "GE SL2", "pL")
+        if not first:
+            gat("a", T.XL[:], X[:], T.L16[:], xk + " L16", "XL0 XL1")
+        act(T.LW[:], T.pL[:, 0:64], F.Copy, "pL", "LW")
+        act(T.NL[:], T.pL[:, 0:64], F.Identity, "pL", "NL", bias=0.5, scale=-1.0)
+
+    nb = [0, NV]
+
+    def blocks(m):
+        for b in range(nb[0], min(NV, nb[0] + m)):
+            o = 8 * (b % 8) + b // 8
+            ts(T.BB[:, 128 * b:128 * b + 128], T.IO[:], T.LW[:, o:o + 1], A.is_equal, "IO LW", "BB%d" % b)
+        nb[0] = min(NV, nb[0] + m)
+
+    def ablocks(m):
+        for b in range(nb[1], min(64, nb[1] + m)):
+            o, w = 8 * (b % 8) + b // 8, 130 * (b - NV)
+            act(T.BT[:, w:w + 129], T.IOX[:, 0:129], F.Sign, "IOX NL", "BB%d" % b, bias=T.NL[:, o:o + 1])
+        nb[1] = min(64, nb[1] + m)
+
+    def round_start(n, X, xk):
+        if n == 0:
+            lst, lk = T.ED, "ED"
+        else:
+            lst, lk = T["LP%d" % (n - 1)], "LP%d" % (n - 1)
+            landed("r%d" % (n - 1), lk)
+        gat("v", T.XL[:, 0:512], X[:], lst[:, 64:96], xk + " " + lk, "XL0")
+        gat("a", T.XL[:, 512:1024], X[:], lst[:, 96:128], xk + " " + lk, "XL1")
+        cp(T.PF2[:], lst[:], lk, "PF2")
+        signs(X, xk, lst, lk)
+        tt(T.D[:], T.PF2[:, 0:64], T.PF2[:, 64:128], A.subtract, "PF2", "D")
+        clip()
+        mm(T.pV[:, 0:64], T.I32N[:], T.D[:], True, False, "I32N D", "pV")
+        ext(T.pV, "pV", T.SELM, "SELM", T.SG, "SG0 SG1", False)
+        ms(T.NA[:], 0.0, "NA")
+        ms(T.DN[:], 0.0, "DN")
+        if n < 2:
+            if n == 1:
+                landed("re", "EDN")
+            e = T.ED if n == 0 else T.EDN
+            cp(T.EF[:], e[:], "ED" if n == 0 else "EDN", "EF")
+        ts(T.UP[:], T.pV[:, 0:64], 0.0, A.is_gt, "pV", "UP")
+        tt(T.T1[:], T.UP[:], T.D[:], A.mult, "UP D", "T1")
+        tt(T.L[:], T.PF2[:, 0:64], T.T1[:], A.subtract, "T1 PF2", "L")
+        tt(T.H[:], T.T1[:], T.PF2[:, 64:128], A.add, "T1 PF2", "H")
+        cp(T.L16[:], T.L[:], "L", "L16")
+        cp(T.H16[:], T.H[:], "H", "H16")
+        digits(X, xk, True)
+
+    def step(n, k, X, xk):
+        last = k == ST - 1
+        nb[0], nb[1] = 0, NV
+        if k == 0:
+            gat("v", T.GS[:], T.SW[:, 0:3072], T.H16[:], SW + " H16", "GS0 GS1")
+        else:
+            gat("v", T.GS[:, 0:512], T.SW[:, 0:3072], T.H16[:, 0:32], SW + " H16", "GS0")
+            gat("a", T.GS[:, 512:1024], T.SW[:, 0:3072], T.H16[:, 32:64], SW + " H16", "GS1")
+            ablocks(M1)
+        if n == 0 and k == 0:
+            late_constants()
+            act(T.SELF[:], T.SELM[:], F.Identity, "SELM WF", "SELF", scale=T.WF[:])
+        ts(T.OI[:], T.H[:], 255, A.bitwise_and, "H", "OI")
+        if k > 0:
+            ts(T.NS[:], T.pX[:, 0:64], 0.0, A.is_ge, "pX", "NS")
+            tt(T.SD[:], T.SO[:], T.EH[:], A.mult, "SO EH", "SD")
+        cp(T.OF16[:], T.OI[:], "OI", "OF16")
+        if k > 0:
+            tt(T.SIT[:], T.AB[:], T.NS[:], A.mult, "AB NS", "SIT")
+            tt(T.DN[:], T.DN[:], T.SD[:], A.max, "DN SD", "DN")
+        ext(T.pS, "pS", T.SELS, "SELS", T.GS, "GS0 GS1", True)
+        blocks(2)
+        if k > 0:
+            tt(T.NA[:], T.SIT[:], T.DN[:], A.max, "SIT DN", "NA")
+        blocks(N1 - 2)
+        cp(T.S16[:], T.pS[:, 0:64], "pS", "S16")
+        tt(T.D[:], T.pS[:, 0:64], T.L[:], A.subtract, "pS L", "D")
+        signs(X, xk, T.S16, "S16")
+        ablocks(M2)
+        tt(T.SH[:], T.pS[:, 0:64], T.H[:], A.subtract, "pS H", "SH")
+        ts(T.EL[:], T.D[:], 0.0, A.is_equal, "D", "EL", 4096.0, A.mult)
+        clip()
+        ts(T.EH[:], T.SH[:], 0.0, A.is_equal, "SH", "EH", 4096.0, A.mult)
+        mm(T.pV[:, 0:64], T.I32N[:], T.D[:], True, False, "I32N D", "pV")
+        mm(T.pV[:, 0:64], T.IDL[:], T.NA[:], False, False, "IDL NA", "pV")
+        mm(T.pV[:, 0:64], T.IDL[:], T.EL[:], False, False, "IDL EL", "pV")
+        mm(T.pV[:, 0:64], T.IDE[:], T.EH[:], False, False, "IDE EH", "pV")
+        ext(T.pV, "pV", T.SELM, "SELM", T.SG, "SG0 SG1", False)
+        tt(T.NM[:], T.NA[:], T.EL[:], A.max, "NA EL", "NM")
+        tt(T.LH[:], T.SH[:], T.D[:], A.subtract, "SH D", "LH")
+        blocks(N2)
+        ts(T.N3[:], T.pV[:, 0:64], 0.0, A.is_gt, "pV", "N3", 3072.0, A.mult)
+        tt(T.HX[:], T.N3[:], T.H[:], A.max, "N3 H", "HX")
+        cp(T.HX16[:], T.HX[:], "HX", "HX16")
+        e = 128 * EC
+        gat("v", T.AR[:, 0:e], T.OH[:], T.HX16[:, 0:8 * EC], "OH HX16", "AR0")
+        gat("a", T.AR[:, e:1024], T.OH[:], T.HX16[:, 8 * EC:64], "OH HX16", "AR1")
+        for c in range(EC, 8):
+            tr(T.pT1[:, 128 * (c - EC):128 * (c - EC) + 128], T.AR[:, 128 * c:128 * c + 128], "AR1", "pT1")
+        for c in range(EC):
+            tr(T.pT0[:, 128 * c:128 * c + 128], T.AR[:, 128 * c:128 * c + 128], "AR0", "pT0")
+        tt(T.WK[:], T.N3[:], T.NM[:], A.is_gt, "N3 NM", "WK")
+        tt(T.DN[:], T.DN[:], T.EL[:], A.max, "DN EL", "DN")
+        cp(T.AT[:, 0:e], T.pT0[:, 0:e], "pT0", "AT0")
+        act(T.AT[:, e:1024], T.pT1[:, 0:1024 - e], F.Copy, "pT1", "AT1")
+        ablocks(64)
+        blocks(64)
+        for b in range(64):
+            if b == 16:
+                for c in range(8):
+                    mm(T.pL[:, NW * c:NW * c + NW], T.AR[:, 128 * c:128 * c + 128], T.IDN[:, 2 * NV:128], True, True,
+                       "IDN AR%d" % (c >= EC), "pL")
+                act(T.AN[:], T.pL[:, 0:8 * NW], F.Copy, "pL", "AN")
+                gat("a", T.LD[:], T.CT[:], T.L16[:], CT + " L16", "LD")
+            gr, c = b // 8, b % 8
+            o, at = T.pH[:, 16 * gr:16 * gr + 16], T.AT[:, 128 * c + 16 * gr:128 * c + 16 * gr + 16]
+            ky = "BB%d AT%d" % (b, c >= EC)
+            if b < NV:
+                mm(o, T.BB[:, 128 * b:128 * b + 128], at, c == 0, c == 7, ky, "pH")
+            else:
+                w, a = 130 * (b - NV), NW * c + 16 * (gr - NV // 8)
+                mm(o, T.BT[:, w + 1:w + 129], at, c == 0, False, ky, "pH")
+                mm(o, T.BT[:, w:w + 128], T.AN[:, a:a + 16], False, c == 7, "BB%d AN" % b, "pH")
+        tt(T.T1[:], T.WK[:], T.SH[:], A.mult, "WK SH", "T1")
+        if not last:
+            ts(T.AK[:], T.N3[:], 0.0, A.is_equal, "N3", "AK")
+        tt(T.H1[:], T.H[:], T.T1[:], A.add, "H T1", "H1")
+        if not last:
+            z = (ST * n + k + 1) % LB
+            tt(T.AB[:], T.AK[:], T.BITS[:, 64 * z:64 * z + 64], A.mult, "AK BITS%d" % z, "AB")
+        ts(T.C1[:], T.pH[:, 0:128], 1.0 / 2048, A.mult, "pH", "C1", -0.25, A.add)
+        ts(T.C0[:], T.C1[:], 2048.0, A.mult, "C1", "C0", 1.0, A.add)
+        ts(T.FL1[:], T.C1[:], 1.0, A.is_equal, "C1", "FL1")
+        tt(T.FL0[:], T.pH[:, 0:128], T.C0[:], A.is_equal, "pH C0", "FL0")
+        m = 16 * GP
+        mm(T.pS[:, 0:1024 - m], T.IDP[:], T.AR[:, m:1024], True, False, "IDP AR0 AR1", "pS")
+        tr(T.pF[:, 128:256], T.FL1[:], "FL1", "pF")
+        tr(T.pF[:, 0:128], T.FL0[:], "FL0", "pF")
+        cp(T.FT[:], T.pF[:, 0:256], "pF", "FT")
+        tt(T.GF[:, 0:m], T.FT[:].indirect(T.OF16[:, 0:GP]), T.AR[:, 0:m], A.mult, "FT OF16 AR0 AR1", "GF0")
+        gat("a", T.XS[:, 512:1536 - m], T.FT[:], T.OF16[:, GP:64], "FT OF16", "XS1")
+        mm(T.pX[:, 0:64], T.I32P[:], T.TR[:], True, False, "I32P TR", "pX")
+        mm(T.pS[:, 0:1024 - m], T.IDF[:], T.XS[:, 512:1536 - m], False, True, "IDF XS1", "pS")
+        act(T.GF[:, m:1024], T.pS[:, 0:1024 - m], F.Relu, "pS", "GF1", bias=-4096.0)
+        ext(T.pX, "pX", T.SELF, "SELF", T.GF, "GF0 GF1", False)
+        tt(T.SC[:], T.pX[:, 0:64], T.H[:], A.max, "pX H", "SC")
+        final = last and n == RO - 1
+        if not final:
+            ts(T.SO[:], T.pX[:, 0:64], 0.0, A.is_lt, "pX", "SO")
+        cp(T.SC16[:], T.SC[:], "SC", "SC16")
+        if not final:
+            tt(T.SE[:], T.SO[:], T.EH[:], A.is_gt, "SO EH", "SE")
+            tt(T.T2[:], T.SE[:], T.LH[:], A.mult, "SE LH", "T2")
+            tt(T.T3[:], T.SE[:], T.D[:], A.mult, "SE D", "T3")
+            tt(T.H[:], T.H1[:], T.T2[:], A.add, "H1 T2", "H")
+            tt(T.L[:], T.L[:], T.T3[:], A.add, "L T3", "L")
+            if not last:
+                cp(T.H16[:], T.H[:], "H", "H16")
+                cp(T.L16[:], T.L[:], "L", "L16")
+                digits(X, xk, False)
+            else:
+                tt(T.SD[:], T.SO[:], T.EH[:], A.mult, "SO EH", "SD")
+                tt(T.T1[:], T.EF[:, 0:64], T.H[:], A.subtract, "EF H", "T1")
+                tt(T.DN[:], T.DN[:], T.SD[:], A.max, "DN SD", "DN")
+                tt(T.T2[:], T.EF[:, 64:128], T.L[:], A.subtract, "EF L", "T2")
+                ts(T.UP[:], T.DN[:], 1.0 / 4096, A.mult, "DN", "UP")
+                tt(T.SH[:], T.T1[:], T.UP[:], A.mult, "T1 UP", "SH")
+                tt(T.D[:], T.T2[:], T.UP[:], A.mult, "T2 UP", "D")
+                tt(T.H1[:], T.SH[:], T.H[:], A.add, "SH H", "H1")
+                tt(T.T3[:], T.D[:], T.L[:], A.add, "D L", "T3")
+                sp = "SP%d" % n
+                cp(T[sp][:, 0:64], T.H1[:], "H1", "+" + sp)
+                cp(T[sp][:, 64:128], T.T3[:], "T3", "+" + sp)
+                send(T["LP%d" % n][:], T[sp][:], "r%d" % n, "s%d" % n, sp)
+        em("v", lambda: g.vector.tensor_copy(T.SW[:].indirect(T.SC16[:]), T.LD[:]), "SC16 LD", SW)
+        if last:
+            act(T.XP[:], X[:, 0:1536], F.Identity, xk, "XP", bias=1.0)
+            act(T.XM[:], X[:, 0:1536], F.Identity, xk, "XM", bias=-1.0)
+
+    def round_end(n, X, xk, Y, yk):
+        final = n == RO - 1
+        if final:
+            dma("s", T.D0[:], T.SW[0:128:16, 0:3072], SW, "D0")
+            dma("s", T.D1[:], T.SW[1:128:16, 0:3072], SW, "D1")
+        bank = ("pH", "pL", "pX")
+        for c in range(3):
+            mm(T[bank[c]][:], T.IDN[:], X[:, 1536 + 512 * c:2048 + 512 * c], True, False, "IDN " + xk, bank[c])
+        ext(T.pS, "pS", T.SELS, "SELS", T.SW, SW, True, 96, 96)
+        cp(T.SL16[:, 96:192], T.pS[:, 0:96], "pS", "SLb")
+        ext(T.pV, "pV", T.SELS, "SELS", T.SW, SW, True, 96, 0)
+        cp(T.SL16[:, 0:96], T.pV[:, 0:96], "pV", "SLa")
+        mm(T.pV[:], T.IDP[:], T.XM[:, 0:512], True, True, "IDP XM", "pV")
+        mm(T.pS[:], T.IDP[:], T.XM[:, 512:1024], True, True, "IDP XM", "pS")
+
+        def ga(c):
+            gat("a", T.XS[:, 512 * c:512 * c + 512], X[:], T.SL16[:, 96 + 32 * c:128 + 32 * c], xk + " SLb", "XS%d" % c)
+            mm(T[bank[c]][:], T.IDP[:], T.XS[:, 512 * c:512 * c + 512], False, True, "IDP XS%d" % c, bank[c])
+
+        def sg(c):
+            act(T.SN[:, 512 * c:512 * c + 512], T[bank[c]][:], F.Sign, bank[c], "SN%d" % c)
+            o = 1536 + 512 * c
+            mm(T[bank[c]][:], T.IDP[:], X[:, o:o + 512], True, False, "IDP " + xk, bank[c])
+            mm(T[bank[c]][:], T.IDP[:], T.SN[:, 512 * c:512 * c + 512], False, True, "IDP SN%d" % c, bank[c])
+
+        def ev(c):
+            o = 1536 + 512 * c
+            act(Y[:, o:o + 512], T[bank[c]][:], F.Copy, bank[c], "+" + yk + "b")
+        ga(0), ga(1), sg(0), ga(2), sg(1), ev(0), sg(2), ev(1), ev(2)
+        tt(T.DD[:], X[:].indirect(T.SL16[:, 0:96]), T.XP[:], A.min, xk + " SLa XP", "DD")
+        tt(Y[:, 0:512], T.DD[:, 0:512], T.pV[:], A.max, "DD pV", "+" + yk + "a")
+        tt(Y[:, 512:1024], T.DD[:, 512:1024], T.pS[:], A.max, "DD pS", "+" + yk + "a")
+        tt(Y[:, 1024:1536], T.DD[:, 1024:1536], T.XM[:, 1024:1536], A.max, "DD XM", "+" + yk + "a")
+        if final:
+            dma("s", T.yx[:, 0:1536], Y[:, 0:1536], yk + "a", "oxa")
+            dma("a", T.yx[:, 1536:3072], Y[:, 1536:3072], yk + "b", "oxb")
+            ts(T.Y2[:], T.D0[:], 64.0, A.mult, "D0", "Y2")
+            tt(T.Y3[:], T.Y2[:], T.D1[:], A.add, "Y2 D1", "Y3")
+            dma("s", T.ys[:], T.Y3[:], "Y3", "oy")
+
+    X, Y, xk, yk = T.XA, T.XB, "X0", "X1"
+    for n in range(RO):
+        xr = xk + "a " + xk + "b"
+        round_start(n, X, xr)
+        for k in range(ST):
+            step(n, k, X, xr)
+        round_end(n, X, xr, Y, yk)
+        X, Y, xk, yk = Y, X, yk, xk
+    for s, v in total.items():
+        if seen["g"].get(s, 0) < v:
+            g.wait_ge(T.sem[s], v)

@@ -1,20 +1,17 @@
 from concourse.mybir import AluOpType as A, ActivationFunctionType as F
 
 RO, ST, LB = 3, 4, 10
-BIG = 131072.0
-BS, GP, EC = 36, 48, 5
-NV = 56
-NW = 128 - 2 * NV
-N1, N2, M1, M2 = 7, 8, 4, 4
+BIG, ROOT, TOP = 131072.0, 3072, 3073
+BS, GP = 40, 46
+NV = 52
 DT = {"b": "bfloat16", "f": "float32", "i": "int32", "u": "uint16"}
-SCRATCH = {"BB": ("sbuf", [128, 128 * NV], "bfloat16"), "BT": ("sbuf", [128, 130 * (64 - NV)], "bfloat16"),
-           "AN": ("sbuf", [128, 8 * NW], "bfloat16")}
-for _t in ("b3072 XA XB CT;b4096 SW;b3088 OH;b1024 GE GS XL LD SG AR AT GF;b1536 DD XS SN XP XM;"
-           "b64 LW;f64 NL;b128 FL0 FL1 BD IO IDP IDN IDE IDL IDF;b130 IOX;b256 FT WR;i128 C1 FI EI;f128 C0 I32P I32N EF PF2;"
-           "b2048 SELS SELM SELF;b8 SL2;i1 PI GI QI;f1 PF GFC QF GC WS WT WF WH;f16 EQ EQW;i192 UI VI W1 W2 W3 V1 V2 SI;"
-           "b192 D0 D1 D2 S0 S1;f192 Y2 Y3;u192 SL16;i64 LI LN H OI;i640 BI;b640 BITS;u128 ED EDN LP0 LP1 SP0 SP1;"
-           "f64 TR L D SH N3 HX WK T1 H1 LH AK AB SC SO SE T2 T3 NS UP;u64 H16 L16 S16 OF16 HX16 SC16;"
-           "b64 EH EL NM NA DN SD SIT").split(";"):
+SCRATCH = {"BT": ("sbuf", [128, 128 * (64 - NV)], "bfloat16")}
+for _t in ("b3088 XA XB CT DG;b4112 SW;b1024 GE GS XL LD SG AT GF;b1536 DD XS SN XP XM;b8192 BB;"
+           "b64 AK2;f64 DL AKN;b128 FL0 FL1 BD IO IDP IDN IDF;b256 WR;b272 FT;i128 C1 FI EI;f128 C0 I32P I32N EF PF2;"
+           "b2048 SELS SELM SELF;b8 M2 S2P S2N;i1 PI GI QI;f1 PF GFC QF GC WS WT WF;f16 EQ;i192 UI VI LV W1 W2 W3 V1 V2 SI;"
+           "b192 D0 D1 D2 S0 S1;f192 Y2 Y3 VM VK;u192 SL16;i64 LN H OI BI;u128 ED EDN LP0 LP1 SP0 SP1;"
+           "f64 TR L D SH T1 H1 LH L1 OF SC SO T2 T3 NS UP N3 AK WK EL AB SIT G R1 R2 R3;"
+           "u64 G16 L16 S16 OF16 SC16").split(";"):
     for _n in _t.split()[1:]:
         SCRATCH[_n] = ("sbuf", [128, int(_t.split()[0][1:])], DT[_t[0]])
 for _n in ("pS", "pV", "pX", "pL", "pH"):
@@ -23,7 +20,6 @@ for _n in ("pT0", "pT1", "pF"):
     SCRATCH[_n] = ("psum", [128, 1024], "bfloat16")
 PS = ("pS", "pV", "pX", "pL", "pH", "pT0", "pT1", "pF")
 SEMAPHORES = ["cv", "ca", "cp", "cg", "se", "s0", "s1", "re", "r0", "r1"] + ["d%d" % i for i in range(24)]
-CT = "CT CT0 CT1 CT2"
 SW = "SW SWh SWl"
 
 
@@ -115,6 +111,9 @@ def rank_program(g, core, T, topo):
         else:
             em("v", lambda: g.vector.tensor_scalar(out, a, s1, s2, op0, op1), rd, wr)
 
+    def t3(o, a, b, op):
+        tt(T[o][:], T[a][:], T[b][:], op, a + " " + b, o)
+
     def ms(ap, c, wr):
         em("v", lambda: g.vector.memset(ap, c), "", wr)
 
@@ -133,117 +132,120 @@ def rank_program(g, core, T, topo):
         else:
             act(out, win.indirect(off), F.Copy, rd, wr)
 
-    def ext(ps, key, sel, selkey, src, rd, start, n=64, o=0):
+    def ext(ps, key, sel, src, rd, start, n=64, o=0):
         for q in range(16):
-            mm(ps[:, 0:n], sel[:, q * 128:(q + 1) * 128], src[:, 16 * o + q:16 * (o + n):16], start and q == 0, q == 15,
-               rd + " " + selkey, key)
+            mm(ps[:, 0:n], T[sel][:, q * 128:(q + 1) * 128], src[:, 16 * o + q:16 * (o + n):16], start and q == 0, q == 15,
+               rd + " " + sel, key)
 
     dma("s", T.EI[:, 0:64], T.ea[:], "", "EIa")
     dma("a", T.EI[:, 64:128], T.eb[:], "", "EIb")
     dma("a", T.SI[:], T.succ[:], "", "SI")
-    dma("s", T.XA[:], T.x[:], "", "X0a X0b")
+    dma("s", T.XA[:, 0:3072], T.x[:], "", "X0a X0b X0c X0d")
 
-    def iota(ap, pat, base, cm, wr, **kw):
-        em("g", lambda: g.iota(ap, pat, base, cm, **kw), "", wr)
-    iota(T.PI[:], [[1, 1]], 0, 1, "PI")
-    iota(T.FI[:], [[1, 128]], 0, 0, "FI")
-    iota(T.UI[:], [[1, 192]], 0, 192, "UI")
-    iota(T.LI[:], [[16, 64]], 0, 0, "LI")
-    iota(T.IOX[:], [[1, 130]], -1, 0, "IOX", allow_small_or_imprecise_dtypes=True)
-    ms(T.SELM[:], 0.0, "SELM")
+    def iota(ap, pat, cm, wr, **kw):
+        em("g", lambda: g.iota(ap, pat, 0, cm, **kw), "", wr)
+    iota(T.PI[:], [[1, 1]], 1, "PI")
+    iota(T.FI[:], [[1, 128]], 0, "FI")
+    iota(T.UI[:], [[1, 192]], 192, "UI")
+    iota(T.LV[:], [[16, 192]], 0, "LV")
+    iota(T.DG[:], [[0, 3088]], 0, "DG DG0 DG1", allow_small_or_imprecise_dtypes=True)
+    ms(T.GS[:], 0.0, "GS0 GS1")
+    for c in range(3):
+        act(T.SW[:, 1024 * c:1024 * c + 1024], T.GS[:], F.Copy, "GS0 GS1", "+SW +SWh +SWl")
     ts(T.GI[:], T.PI[:], 4, A.arith_shift_right, "PI", "GI")
     ts(T.QI[:], T.PI[:], 15, A.bitwise_and, "PI", "QI")
-    cp(T.PF[:], T.PI[:], "PI", "PF")
-    ts(T.C1[:], T.FI[:], 4, A.arith_shift_right, "FI", "C1")
+    ms(T.SELM[:], 0.0, "SELM")
     cp(T.GFC[:], T.GI[:], "GI", "GFC")
     cp(T.QF[:], T.QI[:], "QI", "QF")
-    cp(T.IO[:], T.FI[:], "FI", "IO")
-    ts(T.BD[:], T.C1[:], T.GFC[:], A.is_equal, "C1 GFC", "BD", 4096.0, A.mult)
-    ts(T.EQ[:], T.FI[:, 0:16], T.QF[:], A.is_equal, "FI QF", "EQ")
+    ts(T.C1[:], T.FI[:], 4, A.arith_shift_right, "FI", "C1")
     ts(T.GC[:], T.GFC[:], -3072.0, A.mult, "GFC", "GC")
-    ms(T.SW[:], 0.0, SW)
-    ts(T.WF[:], T.QF[:], 11.5, A.is_lt, "QF", "WF", -BIG / 4096, A.mult)
+    ts(T.EQ[:], T.FI[:, 0:16], T.QF[:], A.is_equal, "FI QF", "EQ")
+    ts(T.BD[:], T.C1[:], T.GFC[:], A.is_equal, "C1 GFC", "BD", 4096.0, A.mult)
     ts(T.VI[:], T.UI[:], T.GC[:], A.add, "UI GC", "VI")
-    ts(T.WS[:], T.EQ[:, 0:1], 64.0 / 4096, A.mult, "EQ", "WS")
-    for q in range(16):
-        cp(T.SELM[:, q * 128 + q:(q + 1) * 128:16], T.BD[:, 0:128:16], "BD", "SELM" if q == 0 else "+SELM")
-    ts(T.WT[:], T.EQ[:, 1:2], 1.0 / 4096, A.mult, "EQ WS", "WT", T.WS[:], A.add)
-    cp(T.ED[:], T.EI[:], "EIa EIb", "ED")
-    send(T.EDN[:], T.ED[:], "re", "se", "ED")
-    ts(T.W1[:], T.SI[:], 6, A.arith_shift_right, "SI", "W1")
-    ts(T.W2[:], T.SI[:], 63, A.bitwise_and, "SI", "W2")
+    ts(T.VK[:], T.VI[:], -1.0, A.mult, "VI", "VK", float(ROOT), A.add)
+    tt(T.Y2[:], T.SI[:], T.VI[:], A.is_equal, "SI VI", "Y2")
+    tt(T.Y3[:], T.Y2[:], T.VK[:], A.mult, "Y2 VK", "Y3")
+    tt(T.W3[:], T.Y3[:], T.SI[:], A.add, "Y3 SI", "W3")
+    ts(T.W1[:], T.W3[:], 6, A.arith_shift_right, "W3", "W1")
+    ts(T.W2[:], T.W3[:], 63, A.bitwise_and, "W3", "W2")
     cp(T.S0[:], T.W1[:], "W1", "S0")
     cp(T.S1[:], T.W2[:], "W2", "S1")
-    act(T.SELS[:], T.SELM[:], F.Identity, "SELM WT", "SELS", scale=T.WT[:])
     dma("s", T.SW[0:128:16, 0:3072], T.S0[:], "S0", "SWh")
     dma("s", T.SW[1:128:16, 0:3072], T.S1[:], "S1", "SWl")
-    ms(T.CT[:], 0.0, CT)
-    ts(T.V1[:], T.VI[:], 6, A.arith_shift_right, "VI", "V1")
-    ts(T.V2[:], T.VI[:], 63, A.bitwise_and, "VI", "V2")
-    ts(T.W3[:], T.VI[:], 127, A.bitwise_and, "VI", "W3")
-    cp(T.D2[:], T.W3[:], "W3", "D2")
-    cp(T.D0[:], T.V1[:], "V1", "D0")
-    cp(T.D1[:], T.V2[:], "V2", "D1")
-    for k in (2, 0, 1):
-        dma("s", T.CT[k:128:16, :], T["D%d" % k][:], "D%d" % k, "CT%d" % k)
+    cp(T.ED[:], T.EI[:], "EIa EIb", "ED")
+    send(T.EDN[:], T.ED[:], "re", "se", "ED")
+    for q in range(16):
+        cp(T.SELM[:, q * 128 + q:(q + 1) * 128:16], T.BD[:, 0:128:16], "BD", "SELM" if q == 0 else "+SELM")
+    ts(T.WS[:], T.EQ[:, 0:1], 64.0 / 4096, A.mult, "EQ", "WS")
+    cp(T.PF[:], T.PI[:], "PI", "PF")
+    for b in "AB":
+        ms(T["X" + b][:, 3072:3088], -1.0, "X%de" % (b == "B"))
+    ts(T.WT[:], T.EQ[:, 1:2], 1.0 / 4096, A.mult, "EQ WS", "WT", T.WS[:], A.add)
+    for b in "AB":
+        ms(T["X" + b][:, TOP:3088], 256.0, "X%de" % (b == "B"))
     for nm, sc in (("IDN", -1.0), ("IDP", 1.0), ("I32N", -1.0)):
         ts(T[nm][:], T.FI[:], T.PF[:], A.is_equal, "FI PF", nm, sc, A.mult)
-    ts(T.SL2[:], T.BD[:, 0:128:16], T.EQ[:, 2:3], A.mult, "BD EQ", "SL2", 1.0 / 4096, A.mult)
+
+    def more_constants():
+        act(T.SELS[:], T.SELM[:], F.Identity, "SELM WT", "SELS", scale=T.WT[:])
+        ms(T.SW[:, 3072:3088], 0.0, "+SW")
+        ts(T.W1[:], T.VI[:], 127, A.bitwise_and, "VI", "W1")
+        ts(T.V1[:], T.VI[:], 6, A.arith_shift_right, "VI", "V1")
+        ts(T.V2[:], T.VI[:], 63, A.bitwise_and, "VI", "V2")
+        ts(T.SW[:, ROOT:ROOT + 1], T.EQ[:, 0:1], 48.0, A.mult, "EQ", "SW")
+        cp(T.D2[:], T.W1[:], "W1", "D2")
+        cp(T.D0[:], T.V1[:], "V1", "D0")
+        cp(T.D1[:], T.V2[:], "V2", "D1")
+        ts(T.SW[:, TOP:TOP + 1], T.EQ[:, 0:1], 48.0, A.mult, "EQ", "SW", T.EQ[:, 1:2], A.add)
+        ts(T.DG[:, ROOT:ROOT + 1], T.EQ[:, 0:1], 48.0, A.mult, "EQ", "DG")
+        dma("s", T.DG[0:128:16, 0:3072], T.D0[:], "D0", "DG0")
+        dma("s", T.DG[1:128:16, 0:3072], T.D1[:], "D1", "DG1")
 
     def late_constants():
-        for nm, sc in (("IDE", -BIG / 4096), ("IDL", 4 * BIG / 4096), ("IDF", 4096.0), ("I32P", 1.0)):
-            ts(T[nm][:], T.FI[:], T.PF[:], A.is_equal, "FI PF", nm, sc, A.mult)
         ms(T.WR[:, 0:128], 1.0, "+WR")
         ms(T.WR[:, 128:256], 2048.0, "+WR")
-        ms(T.OH[:, 3072:3088], 0.0, "+OH")
-        ts(T.WH[:], T.PF[:], 2.0 * NV - 0.5, A.is_gt, "PF", "WH", -0.5, A.mult)
-        ts(T.LN[:], T.LI[:], T.QF[:], A.add, "LI QF", "LN")
-        ts(T.EQW[:], T.EQ[:], T.WH[:], A.mult, "EQ WH", "EQW")
-        ts(T.TR[:], T.LN[:], 3072.0, A.add, "LN", "TR")
-        tt(T.EQW[:], T.EQ[:], T.EQW[:], A.add, "EQ EQW", "EQW")
+        ms(T.CT[:, 3072:3088], 0.0, "+CT +CTl")
         for k in range(12):
-            ts(T.OH[:, 256 * k:256 * k + 256], T.WR[:], T.EQW[:, k:k + 1], A.mult, "WR EQW", "+OH")
-        zs = sorted({(ST * n + k) % LB for n in range(RO) for k in range(1, ST)})
-        for z in zs:
-            ts(T.BI[:, 64 * z:64 * z + 64], T.LN[:], z, A.arith_shift_right, "LN", "BI%d" % z, 1, A.bitwise_and)
-        for z in zs:
-            ts(T.BITS[:, 64 * z:64 * z + 64], T.BI[:, 64 * z:64 * z + 64], 4096.0, A.mult, "BI%d" % z, "BITS%d" % z)
+            ts(T.CT[:, 256 * k:256 * k + 256], T.WR[:], T.EQ[:, k:k + 1], A.mult, "WR EQ", "+CT +CTl")
+        dma("s", T.CT[12:128:16, 0:3072], T.D2[:], "D2", "CTl")
+        cp(T.M2[:], T.BD[:, 0:128:16], "BD", "M2")
+        ts(T.S2P[:], T.BD[:, 0:128:16], T.WT[:], A.mult, "BD WT", "S2P")
+        ts(T.S2N[:], T.BD[:, 0:128:16], T.WT[:], A.mult, "BD WT", "S2N", -1.0, A.mult)
+        cp(T.IO[:], T.FI[:], "FI", "IO")
+
+    def last_constants():
+        ts(T.LN[:], T.LV[:, 0:64], T.QF[:], A.add, "LV QF", "LN")
+        ts(T.WF[:], T.QF[:], 11.5, A.is_lt, "QF", "WF", -BIG / 4096, A.mult)
+        for nm, sc in (("IDF", 4096.0), ("I32P", 1.0)):
+            ts(T[nm][:], T.FI[:], T.PF[:], A.is_equal, "FI PF", nm, sc, A.mult)
+        ts(T.TR[:], T.LN[:], 3088.0, A.add, "LN", "TR")
+        ms(T.FT[:, 256:272], 0.0, "FT")
+        ts(T.VM[:], T.LV[:], T.QF[:], A.add, "LV QF", "VM", -float(ROOT), A.add)
+        act(T.SELF[:], T.SELM[:], F.Identity, "SELM WF", "SELF", scale=T.WF[:])
 
     def signs(X, xk, lst, lk):
         m = 16 * BS
-        tt(T.DD[:, 0:m], X[:].indirect(lst[:, 0:BS]), T.XL[:, 0:m], A.subtract, xk + " XL0 XL1 " + lk, "DD")
+        tt(T.DD[:, 0:m], X[:].indirect(lst[:, 0:BS]), T.XL[:, 0:m], A.subtract, xk + " XL0 XL1 " + lk, "DDa")
         gat("a", T.XS[:, 0:1024 - m], X[:], lst[:, BS:64], xk + " " + lk, "XS0")
         mm(T.pH[:, 0:1024 - m], T.IDN[:], T.XL[:, m:1024], True, False, "IDN XL0 XL1", "pH")
         mm(T.pH[:, 0:1024 - m], T.IDP[:], T.XS[:, 0:1024 - m], False, True, "IDP XS0", "pH")
         act(T.SG[:, m:1024], T.pH[:, 0:1024 - m], F.Sign, "pH", "SG1")
 
     def clip():
-        ts(T.SG[:, 0:16 * BS], T.DD[:, 0:16 * BS], 1.0, A.min, "DD", "SG0", -1.0, A.max)
+        ts(T.SG[:, 0:16 * BS], T.DD[:, 0:16 * BS], 1.0, A.min, "DDa", "SG0", -1.0, A.max)
 
-    def digits(X, xk, first):
-        if first:
-            gat("a", T.XL[:], X[:], T.L16[:], xk + " L16", "XL0 XL1")
-        gat("a", T.GE[:], T.CT[:], T.H16[:], CT + " H16", "GE")
+    def own_x(X, xk):
+        gat("a", T.XL[:], X[:], T.L16[:], xk + " L16", "XL0 XL1")
+
+    def digits(e):
+        gat("a", T.GE[:, 0:512], T.CT[:], T.G16[:, 0:32], "CT CTl G16", "GE0")
+        gat(e, T.GE[:, 512:1024], T.CT[:], T.G16[:, 32:64], "CT CTl G16", "GE1")
         for c in range(8):
-            mm(T.pL[:, 8 * c:8 * c + 8], T.GE[:, 128 * c:128 * c + 128], T.SL2[:], True, True, "GE SL2", "pL")
-        if not first:
-            gat("a", T.XL[:], X[:], T.L16[:], xk + " L16", "XL0 XL1")
-        act(T.LW[:], T.pL[:, 0:64], F.Copy, "pL", "LW")
-        act(T.NL[:], T.pL[:, 0:64], F.Identity, "pL", "NL", bias=0.5, scale=-1.0)
+            tr(T["pT%d" % (c // 4)][:, 128 * (c % 4):128 * (c % 4) + 128], T.GE[:, 128 * c:128 * c + 128],
+               "GE%d" % (c // 4), "pT%d" % (c // 4))
 
-    nb = [0, NV]
-
-    def blocks(m):
-        for b in range(nb[0], min(NV, nb[0] + m)):
-            o = 8 * (b % 8) + b // 8
-            ts(T.BB[:, 128 * b:128 * b + 128], T.IO[:], T.LW[:, o:o + 1], A.is_equal, "IO LW", "BB%d" % b)
-        nb[0] = min(NV, nb[0] + m)
-
-    def ablocks(m):
-        for b in range(nb[1], min(64, nb[1] + m)):
-            o, w = 8 * (b % 8) + b // 8, 130 * (b - NV)
-            act(T.BT[:, w:w + 129], T.IOX[:, 0:129], F.Sign, "IOX NL", "BB%d" % b, bias=T.NL[:, o:o + 1])
-        nb[1] = min(64, nb[1] + m)
+    def turned():
+        act(T.AT[:, 512:1024], T.pT1[:, 0:512], F.Copy, "pT1", "AT1")
 
     def round_start(n, X, xk):
         if n == 0:
@@ -253,152 +255,147 @@ def rank_program(g, core, T, topo):
             landed("r%d" % (n - 1), lk)
         gat("v", T.XL[:, 0:512], X[:], lst[:, 64:96], xk + " " + lk, "XL0")
         gat("a", T.XL[:, 512:1024], X[:], lst[:, 96:128], xk + " " + lk, "XL1")
-        cp(T.PF2[:], lst[:], lk, "PF2")
         signs(X, xk, lst, lk)
-        tt(T.D[:], T.PF2[:, 0:64], T.PF2[:, 64:128], A.subtract, "PF2", "D")
         clip()
+        cp(T.PF2[:], lst[:], lk, "PF2")
+        tt(T.D[:], T.PF2[:, 0:64], T.PF2[:, 64:128], A.subtract, "PF2", "D")
         mm(T.pV[:, 0:64], T.I32N[:], T.D[:], True, False, "I32N D", "pV")
-        ext(T.pV, "pV", T.SELM, "SELM", T.SG, "SG0 SG1", False)
-        ms(T.NA[:], 0.0, "NA")
-        ms(T.DN[:], 0.0, "DN")
+        ext(T.pV, "pV", "SELM", T.SG, "SG0 SG1", False)
+        ms(T.SIT[:], 0.0, "SIT")
+        if n == 0:
+            more_constants()
         if n < 2:
             if n == 1:
                 landed("re", "EDN")
             e = T.ED if n == 0 else T.EDN
             cp(T.EF[:], e[:], "ED" if n == 0 else "EDN", "EF")
         ts(T.UP[:], T.pV[:, 0:64], 0.0, A.is_gt, "pV", "UP")
-        tt(T.T1[:], T.UP[:], T.D[:], A.mult, "UP D", "T1")
+        t3("T1", "UP", "D", A.mult)
         tt(T.L[:], T.PF2[:, 0:64], T.T1[:], A.subtract, "T1 PF2", "L")
         tt(T.H[:], T.T1[:], T.PF2[:, 64:128], A.add, "T1 PF2", "H")
         cp(T.L16[:], T.L[:], "L", "L16")
-        cp(T.H16[:], T.H[:], "H", "H16")
-        digits(X, xk, True)
+        cp(T.G16[:], T.H[:], "H", "G16")
+        own_x(X, xk)
 
     def step(n, k, X, xk):
         last = k == ST - 1
-        nb[0], nb[1] = 0, NV
+        final = last and n == RO - 1
         if k == 0:
-            gat("v", T.GS[:], T.SW[:, 0:3072], T.H16[:], SW + " H16", "GS0 GS1")
-        else:
-            gat("v", T.GS[:, 0:512], T.SW[:, 0:3072], T.H16[:, 0:32], SW + " H16", "GS0")
-            gat("a", T.GS[:, 512:1024], T.SW[:, 0:3072], T.H16[:, 32:64], SW + " H16", "GS1")
-            ablocks(M1)
-        if n == 0 and k == 0:
-            late_constants()
-            act(T.SELF[:], T.SELM[:], F.Identity, "SELM WF", "SELF", scale=T.WF[:])
-        ts(T.OI[:], T.H[:], 255, A.bitwise_and, "H", "OI")
-        if k > 0:
-            ts(T.NS[:], T.pX[:, 0:64], 0.0, A.is_ge, "pX", "NS")
-            tt(T.SD[:], T.SO[:], T.EH[:], A.mult, "SO EH", "SD")
-        cp(T.OF16[:], T.OI[:], "OI", "OF16")
-        if k > 0:
-            tt(T.SIT[:], T.AB[:], T.NS[:], A.mult, "AB NS", "SIT")
-            tt(T.DN[:], T.DN[:], T.SD[:], A.max, "DN SD", "DN")
-        ext(T.pS, "pS", T.SELS, "SELS", T.GS, "GS0 GS1", True)
-        blocks(2)
-        if k > 0:
-            tt(T.NA[:], T.SIT[:], T.DN[:], A.max, "SIT DN", "NA")
-        blocks(N1 - 2)
-        cp(T.S16[:], T.pS[:, 0:64], "pS", "S16")
-        tt(T.D[:], T.pS[:, 0:64], T.L[:], A.subtract, "pS L", "D")
-        signs(X, xk, T.S16, "S16")
-        ablocks(M2)
-        tt(T.SH[:], T.pS[:, 0:64], T.H[:], A.subtract, "pS H", "SH")
-        ts(T.EL[:], T.D[:], 0.0, A.is_equal, "D", "EL", 4096.0, A.mult)
-        clip()
-        ts(T.EH[:], T.SH[:], 0.0, A.is_equal, "SH", "EH", 4096.0, A.mult)
-        mm(T.pV[:, 0:64], T.I32N[:], T.D[:], True, False, "I32N D", "pV")
-        mm(T.pV[:, 0:64], T.IDL[:], T.NA[:], False, False, "IDL NA", "pV")
-        mm(T.pV[:, 0:64], T.IDL[:], T.EL[:], False, False, "IDL EL", "pV")
-        mm(T.pV[:, 0:64], T.IDE[:], T.EH[:], False, False, "IDE EH", "pV")
-        ext(T.pV, "pV", T.SELM, "SELM", T.SG, "SG0 SG1", False)
-        tt(T.NM[:], T.NA[:], T.EL[:], A.max, "NA EL", "NM")
-        tt(T.LH[:], T.SH[:], T.D[:], A.subtract, "SH D", "LH")
-        blocks(N2)
-        ts(T.N3[:], T.pV[:, 0:64], 0.0, A.is_gt, "pV", "N3", 3072.0, A.mult)
-        tt(T.HX[:], T.N3[:], T.H[:], A.max, "N3 H", "HX")
-        cp(T.HX16[:], T.HX[:], "HX", "HX16")
-        e = 128 * EC
-        gat("v", T.AR[:, 0:e], T.OH[:], T.HX16[:, 0:8 * EC], "OH HX16", "AR0")
-        gat("a", T.AR[:, e:1024], T.OH[:], T.HX16[:, 8 * EC:64], "OH HX16", "AR1")
-        for c in range(EC, 8):
-            tr(T.pT1[:, 128 * (c - EC):128 * (c - EC) + 128], T.AR[:, 128 * c:128 * c + 128], "AR1", "pT1")
-        for c in range(EC):
-            tr(T.pT0[:, 128 * c:128 * c + 128], T.AR[:, 128 * c:128 * c + 128], "AR0", "pT0")
-        tt(T.WK[:], T.N3[:], T.NM[:], A.is_gt, "N3 NM", "WK")
-        tt(T.DN[:], T.DN[:], T.EL[:], A.max, "DN EL", "DN")
-        cp(T.AT[:, 0:e], T.pT0[:, 0:e], "pT0", "AT0")
-        act(T.AT[:, e:1024], T.pT1[:, 0:1024 - e], F.Copy, "pT1", "AT1")
-        ablocks(64)
-        blocks(64)
-        for b in range(64):
-            if b == 16:
-                for c in range(8):
-                    mm(T.pL[:, NW * c:NW * c + NW], T.AR[:, 128 * c:128 * c + 128], T.IDN[:, 2 * NV:128], True, True,
-                       "IDN AR%d" % (c >= EC), "pL")
-                act(T.AN[:], T.pL[:, 0:8 * NW], F.Copy, "pL", "AN")
-                gat("a", T.LD[:], T.CT[:], T.L16[:], CT + " L16", "LD")
-            gr, c = b // 8, b % 8
-            o, at = T.pH[:, 16 * gr:16 * gr + 16], T.AT[:, 128 * c + 16 * gr:128 * c + 16 * gr + 16]
-            ky = "BB%d AT%d" % (b, c >= EC)
-            if b < NV:
-                mm(o, T.BB[:, 128 * b:128 * b + 128], at, c == 0, c == 7, ky, "pH")
+            gat("v", T.GS[:], T.SW[:, 0:3088], T.G16[:], SW + " G16", "GS0 GS1")
+            if n == 0:
+                late_constants()
             else:
-                w, a = 130 * (b - NV), NW * c + 16 * (gr - NV // 8)
-                mm(o, T.BT[:, w + 1:w + 129], at, c == 0, False, ky, "pH")
-                mm(o, T.BT[:, w:w + 128], T.AN[:, a:a + 16], False, c == 7, "BB%d AN" % b, "pH")
-        tt(T.T1[:], T.WK[:], T.SH[:], A.mult, "WK SH", "T1")
-        if not last:
-            ts(T.AK[:], T.N3[:], 0.0, A.is_equal, "N3", "AK")
-        tt(T.H1[:], T.H[:], T.T1[:], A.add, "H T1", "H1")
-        if not last:
-            z = (ST * n + k + 1) % LB
-            tt(T.AB[:], T.AK[:], T.BITS[:, 64 * z:64 * z + 64], A.mult, "AK BITS%d" % z, "AB")
+                digits("v")
+        else:
+            gat("v", T.GS[:, 0:512], T.SW[:, 0:3088], T.G16[:, 0:32], SW + " G16", "GS0")
+            gat("a", T.GS[:, 512:1024], T.SW[:, 0:3088], T.G16[:, 32:64], SW + " G16", "GS1")
+        ext(T.pS, "pS", "SELS", T.GS, "GS0 GS1", True)
+        gat("v", T.LD[:, 0:512], T.DG[:], T.L16[:, 0:32], "DG DG0 DG1 L16", "LD0")
+        gat("a", T.LD[:, 512:1024], T.DG[:], T.L16[:, 32:64], "DG DG0 DG1 L16", "LD1")
+        cp(T.S16[:], T.pS[:, 0:64], "pS", "S16")
+        signs(X, xk, T.S16, "S16")
+        if n == 0 and k == 0:
+            digits("a")
+        for c in range(8):
+            o = T.pL[:, 8 * c:8 * c + 8]
+            mm(o, T.GS[:, 128 * c:128 * c + 128], T.S2P[:], True, False, "GS0 GS1 S2P", "pL")
+            mm(o, T.LD[:, 128 * c:128 * c + 128], T.S2N[:], False, True, "LD0 LD1 S2N", "pL")
+        clip()
+        for c in range(8):
+            mm(T.pV[:, 8 * c:8 * c + 8], T.SG[:, 128 * c:128 * c + 128], T.M2[:], True, True,
+               "M2 SG%d" % (c >= BS // 8), "pV")
+        cp(T.DL[:], T.pL[:, 0:64], "pL", "DL")
+        tt(T.D[:], T.pS[:, 0:64], T.L[:], A.subtract, "pS L", "D")
+        cp(T.AT[:, 0:512], T.pT0[:, 0:512], "pT0", "AT0")
+        if k == 0:
+            turned()
+        tt(T.SH[:], T.pS[:, 0:64], T.H[:], A.subtract, "pS H", "SH")
+        for b in range(NV, 64):
+            o, w = 128 * (b % 8) + 16 * (b // 8) + 12, 128 * (b - NV)
+            act(T.BT[:, w:w + 128], T.IO[:], F.Abs, "IO AT%d" % (b % 8 // 4), "BT%d" % b, bias=T.AT[:, o:o + 1], scale=-1.0)
+        tt(T.AK2[:], T.pV[:, 0:64], T.DL[:], A.is_lt, "pV DL", "AK2")
+        act(T.AKN[:], T.AK2[:], F.Copy, "AK2", "AKN", scale=-1.0)
+        for b in range(64):
+            gr, c = b // 8, b % 8
+            o, a = 128 * c + 16 * gr + 12, 8 * c + gr
+            bb, ak = T.BB[:, 128 * b:128 * b + 128], T.AK2[:, a:a + 1]
+            if b < NV:
+                em("v", lambda: g.vector.tensor_scalar(bb, T.IO[:], T.AT[:, o:o + 1], ak, A.is_equal, A.mult),
+                   "IO AK2 AT%d" % (c // 4), "BB%d" % b)
+            else:
+                act(bb, T.BT[:, 128 * (b - NV):128 * (b - NV) + 128], F.Relu, "BT%d AK2 AKN" % b, "BB%d" % b,
+                    bias=ak, scale=T.AKN[:, a:a + 1])
+        mm(T.pV[:, 0:64], T.I32N[:], T.D[:], True, False, "I32N D", "pV")
+        ext(T.pV, "pV", "SELM", T.SG, "SG0 SG1", False)
+        for b in range(64):
+            gr, c = b // 8, b % 8
+            mm(T.pH[:, 16 * gr:16 * gr + 16], T.BB[:, 128 * b:128 * b + 128],
+               T.AT[:, 128 * c + 16 * gr:128 * c + 16 * gr + 16], c == 0, c == 7, "BB%d AT%d" % (b, c // 4), "pH")
+        ts(T.OI[:], T.H[:], 255, A.bitwise_and, "H", "OI")
+        ts(T.N3[:], T.pV[:, 0:64], 0.0, A.is_ge, "pV", "N3", 256.0, A.mult)
+        t3("OF", "OI", "N3", A.max)
+        cp(T.OF16[:], T.OF[:], "OF", "OF16")
+        if n == 0 and k == 0:
+            last_constants()
         ts(T.C1[:], T.pH[:, 0:128], 1.0 / 2048, A.mult, "pH", "C1", -0.25, A.add)
         ts(T.C0[:], T.C1[:], 2048.0, A.mult, "C1", "C0", 1.0, A.add)
         ts(T.FL1[:], T.C1[:], 1.0, A.is_equal, "C1", "FL1")
         tt(T.FL0[:], T.pH[:, 0:128], T.C0[:], A.is_equal, "pH C0", "FL0")
         m = 16 * GP
-        mm(T.pS[:, 0:1024 - m], T.IDP[:], T.AR[:, m:1024], True, False, "IDP AR0 AR1", "pS")
+        mm(T.pS[:, 0:1024 - m], T.IDP[:], T.GE[:, m:1024], True, False, "IDP GE1", "pS")
+        mm(T.pX[:, 0:64], T.I32P[:], T.TR[:], True, False, "I32P TR", "pX")
         tr(T.pF[:, 128:256], T.FL1[:], "FL1", "pF")
         tr(T.pF[:, 0:128], T.FL0[:], "FL0", "pF")
-        cp(T.FT[:], T.pF[:, 0:256], "pF", "FT")
-        tt(T.GF[:, 0:m], T.FT[:].indirect(T.OF16[:, 0:GP]), T.AR[:, 0:m], A.mult, "FT OF16 AR0 AR1", "GF0")
+        cp(T.FT[:, 0:256], T.pF[:, 0:256], "pF", "FT")
+        tt(T.GF[:, 0:m], T.FT[:].indirect(T.OF16[:, 0:GP]), T.GE[:, 0:m], A.mult, "FT OF16 GE0 GE1", "GF0")
         gat("a", T.XS[:, 512:1536 - m], T.FT[:], T.OF16[:, GP:64], "FT OF16", "XS1")
-        mm(T.pX[:, 0:64], T.I32P[:], T.TR[:], True, False, "I32P TR", "pX")
         mm(T.pS[:, 0:1024 - m], T.IDF[:], T.XS[:, 512:1536 - m], False, True, "IDF XS1", "pS")
         act(T.GF[:, m:1024], T.pS[:, 0:1024 - m], F.Relu, "pS", "GF1", bias=-4096.0)
-        ext(T.pX, "pX", T.SELF, "SELF", T.GF, "GF0 GF1", False)
+        ext(T.pX, "pX", "SELF", T.GF, "GF0 GF1", False)
+        if not final:
+            t3("WK", "N3", "SIT", A.is_gt)
+            ts(T.EL[:], T.D[:], 0.0, A.is_equal, "D", "EL", float(ROOT), A.mult)
+            t3("T1", "WK", "SH", A.mult)
+            t3("LH", "SH", "D", A.subtract)
+            t3("H1", "H", "T1", A.add)
+            t3("L1", "L", "EL", A.max)
+        if not last:
+            ts(T.BI[:], T.LN[:], (ST * n + k + 1) % LB, A.arith_shift_right, "LN", "BI", 1, A.bitwise_and)
+            ts(T.AK[:], T.N3[:], 0.0, A.is_equal, "N3", "AK", float(TOP), A.mult)
+            t3("AB", "AK", "BI", A.mult)
         tt(T.SC[:], T.pX[:, 0:64], T.H[:], A.max, "pX H", "SC")
-        final = last and n == RO - 1
         if not final:
             ts(T.SO[:], T.pX[:, 0:64], 0.0, A.is_lt, "pX", "SO")
         cp(T.SC16[:], T.SC[:], "SC", "SC16")
+        if not last:
+            ts(T.NS[:], T.pX[:, 0:64], 0.0, A.is_ge, "pX", "NS")
         if not final:
-            tt(T.SE[:], T.SO[:], T.EH[:], A.is_gt, "SO EH", "SE")
-            tt(T.T2[:], T.SE[:], T.LH[:], A.mult, "SE LH", "T2")
-            tt(T.T3[:], T.SE[:], T.D[:], A.mult, "SE D", "T3")
-            tt(T.H[:], T.H1[:], T.T2[:], A.add, "H1 T2", "H")
-            tt(T.L[:], T.L[:], T.T3[:], A.add, "L T3", "L")
+            t3("T2", "SO", "LH", A.mult)
+            t3("T3", "SO", "D", A.mult)
             if not last:
-                cp(T.H16[:], T.H[:], "H", "H16")
+                t3("SIT", "AB", "NS", A.mult)
+            t3("H", "H1", "T2", A.add)
+            t3("L", "L1", "T3", A.add)
+            if not last:
+                t3("G", "H", "SIT", A.max)
                 cp(T.L16[:], T.L[:], "L", "L16")
-                digits(X, xk, False)
+                cp(T.G16[:], T.G[:], "G", "G16")
+                digits("a")
+                own_x(X, xk)
+                turned()
             else:
-                tt(T.SD[:], T.SO[:], T.EH[:], A.mult, "SO EH", "SD")
+                ts(T.UP[:], T.L[:], float(ROOT), A.is_equal, "L", "UP")
                 tt(T.T1[:], T.EF[:, 0:64], T.H[:], A.subtract, "EF H", "T1")
-                tt(T.DN[:], T.DN[:], T.SD[:], A.max, "DN SD", "DN")
                 tt(T.T2[:], T.EF[:, 64:128], T.L[:], A.subtract, "EF L", "T2")
-                ts(T.UP[:], T.DN[:], 1.0 / 4096, A.mult, "DN", "UP")
-                tt(T.SH[:], T.T1[:], T.UP[:], A.mult, "T1 UP", "SH")
-                tt(T.D[:], T.T2[:], T.UP[:], A.mult, "T2 UP", "D")
-                tt(T.H1[:], T.SH[:], T.H[:], A.add, "SH H", "H1")
-                tt(T.T3[:], T.D[:], T.L[:], A.add, "D L", "T3")
+                t3("SH", "T1", "UP", A.mult)
+                t3("D", "T2", "UP", A.mult)
+                t3("H1", "SH", "H", A.add)
+                t3("T3", "D", "L", A.add)
                 sp = "SP%d" % n
                 cp(T[sp][:, 0:64], T.H1[:], "H1", "+" + sp)
                 cp(T[sp][:, 64:128], T.T3[:], "T3", "+" + sp)
                 send(T["LP%d" % n][:], T[sp][:], "r%d" % n, "s%d" % n, sp)
-        em("v", lambda: g.vector.tensor_copy(T.SW[:].indirect(T.SC16[:]), T.LD[:]), "SC16 LD", SW)
+        em("v", lambda: g.vector.tensor_copy(T.SW[:].indirect(T.SC16[:]), T.LD[:]), "SC16 LD0 LD1", SW)
         if last:
             act(T.XP[:], X[:, 0:1536], F.Identity, xk, "XP", bias=1.0)
             act(T.XM[:], X[:, 0:1536], F.Identity, xk, "XM", bias=-1.0)
@@ -409,17 +406,27 @@ def rank_program(g, core, T, topo):
             dma("s", T.D0[:], T.SW[0:128:16, 0:3072], SW, "D0")
             dma("s", T.D1[:], T.SW[1:128:16, 0:3072], SW, "D1")
         bank = ("pH", "pL", "pX")
-        for c in range(3):
+        for c in (1, 2, 0):
             mm(T[bank[c]][:], T.IDN[:], X[:, 1536 + 512 * c:2048 + 512 * c], True, False, "IDN " + xk, bank[c])
-        ext(T.pS, "pS", T.SELS, "SELS", T.SW, SW, True, 96, 96)
-        cp(T.SL16[:, 96:192], T.pS[:, 0:96], "pS", "SLb")
-        ext(T.pV, "pV", T.SELS, "SELS", T.SW, SW, True, 96, 0)
-        cp(T.SL16[:, 0:96], T.pV[:, 0:96], "pV", "SLa")
+
+        def lists(ps, o, key):
+            ts(T.R1[:], T[ps][:, 0:64], float(ROOT), A.is_equal, ps, "R1")
+            tt(T.R2[:], T.R1[:], T.VM[:, o:o + 64], A.mult, "R1 VM", "R2")
+            tt(T.R3[:], T[ps][:, 0:64], T.R2[:], A.add, ps + " R2", "R3")
+            cp(T.SL16[:, o:o + 64], T.R3[:], "R3", key)
+        ext(T.pS, "pS", "SELS", T.SW, SW, True, 64, 128)
+        lists("pS", 128, "SLc")
+        ext(T.pV, "pV", "SELS", T.SW, SW, True, 64, 0)
+        lists("pV", 0, "SLa")
+        ext(T.pS, "pS", "SELS", T.SW, SW, True, 64, 64)
+        tt(T.DD[:, 0:1024], X[:].indirect(T.SL16[:, 0:64]), T.XP[:, 0:1024], A.min, xk + " SLa XP", "DDa")
+        lists("pS", 64, "SLb")
         mm(T.pV[:], T.IDP[:], T.XM[:, 0:512], True, True, "IDP XM", "pV")
         mm(T.pS[:], T.IDP[:], T.XM[:, 512:1024], True, True, "IDP XM", "pS")
 
         def ga(c):
-            gat("a", T.XS[:, 512 * c:512 * c + 512], X[:], T.SL16[:, 96 + 32 * c:128 + 32 * c], xk + " SLb", "XS%d" % c)
+            gat("a", T.XS[:, 512 * c:512 * c + 512], X[:], T.SL16[:, 96 + 32 * c:128 + 32 * c],
+                xk + (" SLc" if c else " SLb"), "XS%d" % c)
             mm(T[bank[c]][:], T.IDP[:], T.XS[:, 512 * c:512 * c + 512], False, True, "IDP XS%d" % c, bank[c])
 
         def sg(c):
@@ -430,22 +437,27 @@ def rank_program(g, core, T, topo):
 
         def ev(c):
             o = 1536 + 512 * c
-            act(Y[:, o:o + 512], T[bank[c]][:], F.Copy, bank[c], "+" + yk + "b")
-        ga(0), ga(1), sg(0), ga(2), sg(1), ev(0), sg(2), ev(1), ev(2)
-        tt(T.DD[:], X[:].indirect(T.SL16[:, 0:96]), T.XP[:], A.min, xk + " SLa XP", "DD")
-        tt(Y[:, 0:512], T.DD[:, 0:512], T.pV[:], A.max, "DD pV", "+" + yk + "a")
-        tt(Y[:, 512:1024], T.DD[:, 512:1024], T.pS[:], A.max, "DD pS", "+" + yk + "a")
-        tt(Y[:, 1024:1536], T.DD[:, 1024:1536], T.XM[:, 1024:1536], A.max, "DD XM", "+" + yk + "a")
+            act(Y[:, o:o + 512], T[bank[c]][:], F.Copy, bank[c], "+" + yk + ("b" if c else "d"))
+        ga(1), ga(2), sg(1), ga(0), sg(2), ev(1), sg(0), ev(2), ev(0)
+        tt(Y[:, 0:512], T.DD[:, 0:512], T.pV[:], A.max, "DDa pV", "+" + yk + "a")
+        tt(Y[:, 512:1024], T.DD[:, 512:1024], T.pS[:], A.max, "DDa pS", "+" + yk + "a")
+        tt(T.DD[:, 1024:1536], X[:].indirect(T.SL16[:, 64:96]), T.XP[:, 1024:1536], A.min, xk + " SLb XP", "DDb")
+        tt(Y[:, 1024:1536], T.DD[:, 1024:1536], T.XM[:, 1024:1536], A.max, "DDb XM", yk + "c")
         if final:
-            dma("s", T.yx[:, 0:1536], Y[:, 0:1536], yk + "a", "oxa")
-            dma("a", T.yx[:, 1536:3072], Y[:, 1536:3072], yk + "b", "oxb")
+            dma("s", T.yx[:, 0:1024], Y[:, 0:1024], yk + "a", "oxa")
             ts(T.Y2[:], T.D0[:], 64.0, A.mult, "D0", "Y2")
             tt(T.Y3[:], T.Y2[:], T.D1[:], A.add, "Y2 D1", "Y3")
+            ts(T.Y2[:], T.Y3[:], float(ROOT), A.is_equal, "Y3", "Y2")
+            tt(T.Y2[:], T.Y2[:], T.VK[:], A.mult, "Y2 VK", "Y2")
+            tt(T.Y3[:], T.Y3[:], T.Y2[:], A.subtract, "Y3 Y2", "Y3")
+            dma("s", T.yx[:, 1024:1536], Y[:, 1024:1536], yk + "c", "oxc")
             dma("s", T.ys[:], T.Y3[:], "Y3", "oy")
+            dma("s", T.yx[:, 2048:3072], Y[:, 2048:3072], yk + "b", "oxb")
+            dma("s", T.yx[:, 1536:2048], Y[:, 1536:2048], yk + "d", "oxd")
 
     X, Y, xk, yk = T.XA, T.XB, "X0", "X1"
     for n in range(RO):
-        xr = xk + "a " + xk + "b"
+        xr = " ".join(xk + c for c in "abcde")
         round_start(n, X, xr)
         for k in range(ST):
             step(n, k, X, xr)

from concourse.mybir import AluOpType as A, ActivationFunctionType as F

RO, ST, LB = 3, 4, 10
BIG, ROOT, TOP = 131072.0, 3072, 3073
BS, GP = 40, 46
NV = 52
DT = {"b": "bfloat16", "f": "float32", "i": "int32", "u": "uint16"}
SCRATCH = {"BT": ("sbuf", [128, 128 * (64 - NV)], "bfloat16")}
for _t in ("b3088 XA XB CT DG;b4112 SW;b1024 GE GS XL LD SG AT GF;b1536 DD XS SN XP XM;b8192 BB;"
           "b64 AK2;f64 DL AKN;b128 FL0 FL1 BD IO IDP IDN IDF;b256 WR;b272 FT;i128 C1 FI EI;f128 C0 I32P I32N EF PF2;"
           "b2048 SELS SELM SELF;b8 M2 S2P S2N;i1 PI GI QI;f1 PF GFC QF GC WS WT WF;f16 EQ;i192 UI VI LV W1 W2 W3 V1 V2 SI;"
           "b192 D0 D1 D2 S0 S1;f192 Y2 Y3 VM VK;u192 SL16;i64 LN H OI BI;u128 ED EDN LP0 LP1 SP0 SP1;"
           "f64 TR L D SH T1 H1 LH L1 OF SC SO T2 T3 NS UP N3 AK WK EL AB SIT G R1 R2 R3;"
           "u64 G16 L16 S16 OF16 SC16").split(";"):
    for _n in _t.split()[1:]:
        SCRATCH[_n] = ("sbuf", [128, int(_t.split()[0][1:])], DT[_t[0]])
for _n in ("pS", "pV", "pX", "pL", "pH"):
    SCRATCH[_n] = ("psum", [128, 512], "float32")
for _n in ("pT0", "pT1", "pF"):
    SCRATCH[_n] = ("psum", [128, 1024], "bfloat16")
PS = ("pS", "pV", "pX", "pL", "pH", "pT0", "pT1", "pF")
SEMAPHORES = ["cv", "ca", "cp", "cg", "se", "s0", "s1", "re", "r0", "r1"] + ["d%d" % i for i in range(24)]
SW = "SW SWh SWl"


def rank_program(g, core, T, topo):
    rank = T.rank_of(core)
    if rank is None:
        return
    N = len(T.cores)
    nxt, prv = T.cores[(rank + 1) % N], T.cores[(rank - 1) % N]
    eng = {"v": g.vector, "a": g.scalar, "p": g.tensor, "g": g, "s": g.sync}
    total, seen, wr_, rd_ = {}, {e: {} for e in eng}, {}, {}

    def need(e, toks):
        best = {}
        for t in toks:
            if t[0] not in best or best[t[0]][1] < t[1]:
                best[t[0]] = t
        for t in sorted(best.values(), key=lambda t: -len(t[3])):
            if seen[e].get(t[0], 0) < t[1]:
                eng[e].wait_ge(T.sem[t[0]], t[1])
                seen[e][t[0]] = t[1]
                for s, v in t[3].items():
                    seen[e][s] = max(seen[e].get(s, 0), v)

    def before(e, rd, wr):
        toks = []
        for k in rd:
            toks += wr_.get(k, {}).values()
            if k in PS:
                toks += [t for t in rd_.get(k, {}).values() if t[2] != e]
        for k in wr:
            part = k[0] == "+" or (e == "p" and k in PS)
            k = k.strip("+")
            toks += [t for t in wr_.get(k, {}).values() if not (part and t[2] == e)]
            toks += rd_.get(k, {}).values()
        need(e, toks)

    def after(tok, rd, wr):
        for k in wr:
            part = k[0] == "+"
            k = k.strip("+")
            if not part:
                wr_[k] = {}
            wr_.setdefault(k, {})[tok[0]] = tok
            rd_[k] = {}
        for k in rd:
            if k not in wr:
                rd_.setdefault(k, {})[tok[0]] = tok

    def em(e, fn, rd, wr):
        rd, wr = rd.split(), wr.split()
        before(e, rd, wr)
        s = "c" + e
        total[s] = total.get(s, 0) + 1
        fn().then_inc(T.sem[s], 1)
        after((s, total[s], e, dict(seen[e])), rd, wr)

    nd = [0]

    def dma(e, out, in_, rd, wr):
        rd, wr = rd.split(), wr.split()
        before(e, rd, wr)
        s = "d%d" % nd[0]
        nd[0] += 1
        total[s] = 16
        eng[e].dma_start(out, in_).then_inc(T.sem[s], 16)
        after((s, 16, "D", dict(seen[e])), rd, wr)

    def send(out, in_, rs, ls, rd):
        before("g", rd.split(), [])
        rid, pid = topo.addr(nxt, core)
        g.remote_dma(out, in_, T.sem[rs], T.sem[ls], pid, rid, topo.mask(core, nxt))
        total[ls] = len(topo.engines(core, nxt))
        total[rs] = len(topo.engines(prv, core))
        after((ls, total[ls], "D", {}), rd.split(), [])

    def landed(rs, key):
        wr_[key] = {rs: (rs, total[rs], "N", {})}

    def cp(out, in_, rd, wr):
        em("v", lambda: g.vector.tensor_copy(out, in_), rd, wr)

    def tt(out, a, b, op, rd, wr):
        em("v", lambda: g.vector.tensor_tensor(out, a, b, op), rd, wr)

    def ts(out, a, s1, op0, rd, wr, s2=None, op1=None):
        if op1 is None:
            em("v", lambda: g.vector.tensor_scalar(out, a, s1, None, op0), rd, wr)
        else:
            em("v", lambda: g.vector.tensor_scalar(out, a, s1, s2, op0, op1), rd, wr)

    def t3(o, a, b, op):
        tt(T[o][:], T[a][:], T[b][:], op, a + " " + b, o)

    def ms(ap, c, wr):
        em("v", lambda: g.vector.memset(ap, c), "", wr)

    def act(out, in_, fn, rd, wr, bias=0.0, scale=1.0):
        em("a", lambda: g.scalar.activation(out, in_, fn, bias=bias, scale=scale), rd, wr)

    def mm(out, l, r, start, stop, rd, wr):
        em("p", lambda: g.tensor.matmul(out, l, r, start, stop), rd, wr)

    def tr(out, in_, rd, wr):
        em("p", lambda: g.tensor.transpose(out, in_, T.IDP[:]), rd + " IDP", wr)

    def gat(e, out, win, off, rd, wr):
        if e == "v":
            cp(out, win.indirect(off), rd, wr)
        else:
            act(out, win.indirect(off), F.Copy, rd, wr)

    def ext(ps, key, sel, src, rd, start, n=64, o=0):
        for q in range(16):
            mm(ps[:, 0:n], T[sel][:, q * 128:(q + 1) * 128], src[:, 16 * o + q:16 * (o + n):16], start and q == 0, q == 15,
               rd + " " + sel, key)

    dma("s", T.EI[:, 0:64], T.ea[:], "", "EIa")
    dma("a", T.EI[:, 64:128], T.eb[:], "", "EIb")
    dma("a", T.SI[:], T.succ[:], "", "SI")
    dma("s", T.XA[:, 0:3072], T.x[:], "", "X0a X0b X0c X0d")

    def iota(ap, pat, cm, wr, **kw):
        em("g", lambda: g.iota(ap, pat, 0, cm, **kw), "", wr)
    iota(T.PI[:], [[1, 1]], 1, "PI")
    iota(T.FI[:], [[1, 128]], 0, "FI")
    iota(T.UI[:], [[1, 192]], 192, "UI")
    iota(T.LV[:], [[16, 192]], 0, "LV")
    iota(T.DG[:], [[0, 3088]], 0, "DG DG0 DG1", allow_small_or_imprecise_dtypes=True)
    ms(T.GS[:], 0.0, "GS0 GS1")
    for c in range(3):
        act(T.SW[:, 1024 * c:1024 * c + 1024], T.GS[:], F.Copy, "GS0 GS1", "+SW +SWh +SWl")
    ts(T.GI[:], T.PI[:], 4, A.arith_shift_right, "PI", "GI")
    ts(T.QI[:], T.PI[:], 15, A.bitwise_and, "PI", "QI")
    ms(T.SELM[:], 0.0, "SELM")
    cp(T.GFC[:], T.GI[:], "GI", "GFC")
    cp(T.QF[:], T.QI[:], "QI", "QF")
    ts(T.C1[:], T.FI[:], 4, A.arith_shift_right, "FI", "C1")
    ts(T.GC[:], T.GFC[:], -3072.0, A.mult, "GFC", "GC")
    ts(T.EQ[:], T.FI[:, 0:16], T.QF[:], A.is_equal, "FI QF", "EQ")
    ts(T.BD[:], T.C1[:], T.GFC[:], A.is_equal, "C1 GFC", "BD", 4096.0, A.mult)
    ts(T.VI[:], T.UI[:], T.GC[:], A.add, "UI GC", "VI")
    ts(T.VK[:], T.VI[:], -1.0, A.mult, "VI", "VK", float(ROOT), A.add)
    tt(T.Y2[:], T.SI[:], T.VI[:], A.is_equal, "SI VI", "Y2")
    tt(T.Y3[:], T.Y2[:], T.VK[:], A.mult, "Y2 VK", "Y3")
    tt(T.W3[:], T.Y3[:], T.SI[:], A.add, "Y3 SI", "W3")
    ts(T.W1[:], T.W3[:], 6, A.arith_shift_right, "W3", "W1")
    ts(T.W2[:], T.W3[:], 63, A.bitwise_and, "W3", "W2")
    cp(T.S0[:], T.W1[:], "W1", "S0")
    cp(T.S1[:], T.W2[:], "W2", "S1")
    dma("s", T.SW[0:128:16, 0:3072], T.S0[:], "S0", "SWh")
    dma("s", T.SW[1:128:16, 0:3072], T.S1[:], "S1", "SWl")
    cp(T.ED[:], T.EI[:], "EIa EIb", "ED")
    send(T.EDN[:], T.ED[:], "re", "se", "ED")
    for q in range(16):
        cp(T.SELM[:, q * 128 + q:(q + 1) * 128:16], T.BD[:, 0:128:16], "BD", "SELM" if q == 0 else "+SELM")
    ts(T.WS[:], T.EQ[:, 0:1], 64.0 / 4096, A.mult, "EQ", "WS")
    cp(T.PF[:], T.PI[:], "PI", "PF")
    for b in "AB":
        ms(T["X" + b][:, 3072:3088], -1.0, "X%de" % (b == "B"))
    ts(T.WT[:], T.EQ[:, 1:2], 1.0 / 4096, A.mult, "EQ WS", "WT", T.WS[:], A.add)
    for b in "AB":
        ms(T["X" + b][:, TOP:3088], 256.0, "X%de" % (b == "B"))
    for nm, sc in (("IDN", -1.0), ("IDP", 1.0), ("I32N", -1.0)):
        ts(T[nm][:], T.FI[:], T.PF[:], A.is_equal, "FI PF", nm, sc, A.mult)

    def more_constants():
        act(T.SELS[:], T.SELM[:], F.Identity, "SELM WT", "SELS", scale=T.WT[:])
        ms(T.SW[:, 3072:3088], 0.0, "+SW")
        ts(T.W1[:], T.VI[:], 127, A.bitwise_and, "VI", "W1")
        ts(T.V1[:], T.VI[:], 6, A.arith_shift_right, "VI", "V1")
        ts(T.V2[:], T.VI[:], 63, A.bitwise_and, "VI", "V2")
        ts(T.SW[:, ROOT:ROOT + 1], T.EQ[:, 0:1], 48.0, A.mult, "EQ", "SW")
        cp(T.D2[:], T.W1[:], "W1", "D2")
        cp(T.D0[:], T.V1[:], "V1", "D0")
        cp(T.D1[:], T.V2[:], "V2", "D1")
        ts(T.SW[:, TOP:TOP + 1], T.EQ[:, 0:1], 48.0, A.mult, "EQ", "SW", T.EQ[:, 1:2], A.add)
        ts(T.DG[:, ROOT:ROOT + 1], T.EQ[:, 0:1], 48.0, A.mult, "EQ", "DG")
        dma("s", T.DG[0:128:16, 0:3072], T.D0[:], "D0", "DG0")
        dma("s", T.DG[1:128:16, 0:3072], T.D1[:], "D1", "DG1")

    def late_constants():
        ms(T.WR[:, 0:128], 1.0, "+WR")
        ms(T.WR[:, 128:256], 2048.0, "+WR")
        ms(T.CT[:, 3072:3088], 0.0, "+CT +CTl")
        for k in range(12):
            ts(T.CT[:, 256 * k:256 * k + 256], T.WR[:], T.EQ[:, k:k + 1], A.mult, "WR EQ", "+CT +CTl")
        dma("s", T.CT[12:128:16, 0:3072], T.D2[:], "D2", "CTl")
        cp(T.M2[:], T.BD[:, 0:128:16], "BD", "M2")
        ts(T.S2P[:], T.BD[:, 0:128:16], T.WT[:], A.mult, "BD WT", "S2P")
        ts(T.S2N[:], T.BD[:, 0:128:16], T.WT[:], A.mult, "BD WT", "S2N", -1.0, A.mult)
        cp(T.IO[:], T.FI[:], "FI", "IO")

    def last_constants():
        ts(T.LN[:], T.LV[:, 0:64], T.QF[:], A.add, "LV QF", "LN")
        ts(T.WF[:], T.QF[:], 11.5, A.is_lt, "QF", "WF", -BIG / 4096, A.mult)
        for nm, sc in (("IDF", 4096.0), ("I32P", 1.0)):
            ts(T[nm][:], T.FI[:], T.PF[:], A.is_equal, "FI PF", nm, sc, A.mult)
        ts(T.TR[:], T.LN[:], 3088.0, A.add, "LN", "TR")
        ms(T.FT[:, 256:272], 0.0, "FT")
        ts(T.VM[:], T.LV[:], T.QF[:], A.add, "LV QF", "VM", -float(ROOT), A.add)
        act(T.SELF[:], T.SELM[:], F.Identity, "SELM WF", "SELF", scale=T.WF[:])

    def signs(X, xk, lst, lk):
        m = 16 * BS
        tt(T.DD[:, 0:m], X[:].indirect(lst[:, 0:BS]), T.XL[:, 0:m], A.subtract, xk + " XL0 XL1 " + lk, "DDa")
        gat("a", T.XS[:, 0:1024 - m], X[:], lst[:, BS:64], xk + " " + lk, "XS0")
        mm(T.pH[:, 0:1024 - m], T.IDN[:], T.XL[:, m:1024], True, False, "IDN XL0 XL1", "pH")
        mm(T.pH[:, 0:1024 - m], T.IDP[:], T.XS[:, 0:1024 - m], False, True, "IDP XS0", "pH")
        act(T.SG[:, m:1024], T.pH[:, 0:1024 - m], F.Sign, "pH", "SG1")

    def clip():
        ts(T.SG[:, 0:16 * BS], T.DD[:, 0:16 * BS], 1.0, A.min, "DDa", "SG0", -1.0, A.max)

    def own_x(X, xk):
        gat("a", T.XL[:], X[:], T.L16[:], xk + " L16", "XL0 XL1")

    def digits(e):
        gat("a", T.GE[:, 0:512], T.CT[:], T.G16[:, 0:32], "CT CTl G16", "GE0")
        gat(e, T.GE[:, 512:1024], T.CT[:], T.G16[:, 32:64], "CT CTl G16", "GE1")
        for c in range(8):
            tr(T["pT%d" % (c // 4)][:, 128 * (c % 4):128 * (c % 4) + 128], T.GE[:, 128 * c:128 * c + 128],
               "GE%d" % (c // 4), "pT%d" % (c // 4))

    def turned():
        act(T.AT[:, 512:1024], T.pT1[:, 0:512], F.Copy, "pT1", "AT1")

    def round_start(n, X, xk):
        if n == 0:
            lst, lk = T.ED, "ED"
        else:
            lst, lk = T["LP%d" % (n - 1)], "LP%d" % (n - 1)
            landed("r%d" % (n - 1), lk)
        gat("v", T.XL[:, 0:512], X[:], lst[:, 64:96], xk + " " + lk, "XL0")
        gat("a", T.XL[:, 512:1024], X[:], lst[:, 96:128], xk + " " + lk, "XL1")
        signs(X, xk, lst, lk)
        clip()
        cp(T.PF2[:], lst[:], lk, "PF2")
        tt(T.D[:], T.PF2[:, 0:64], T.PF2[:, 64:128], A.subtract, "PF2", "D")
        mm(T.pV[:, 0:64], T.I32N[:], T.D[:], True, False, "I32N D", "pV")
        ext(T.pV, "pV", "SELM", T.SG, "SG0 SG1", False)
        ms(T.SIT[:], 0.0, "SIT")
        if n == 0:
            more_constants()
        if n < 2:
            if n == 1:
                landed("re", "EDN")
            e = T.ED if n == 0 else T.EDN
            cp(T.EF[:], e[:], "ED" if n == 0 else "EDN", "EF")
        ts(T.UP[:], T.pV[:, 0:64], 0.0, A.is_gt, "pV", "UP")
        t3("T1", "UP", "D", A.mult)
        tt(T.L[:], T.PF2[:, 0:64], T.T1[:], A.subtract, "T1 PF2", "L")
        tt(T.H[:], T.T1[:], T.PF2[:, 64:128], A.add, "T1 PF2", "H")
        cp(T.L16[:], T.L[:], "L", "L16")
        cp(T.G16[:], T.H[:], "H", "G16")
        own_x(X, xk)

    def step(n, k, X, xk):
        last = k == ST - 1
        final = last and n == RO - 1
        if k == 0:
            gat("v", T.GS[:], T.SW[:, 0:3088], T.G16[:], SW + " G16", "GS0 GS1")
            if n == 0:
                late_constants()
            else:
                digits("v")
        else:
            gat("v", T.GS[:, 0:512], T.SW[:, 0:3088], T.G16[:, 0:32], SW + " G16", "GS0")
            gat("a", T.GS[:, 512:1024], T.SW[:, 0:3088], T.G16[:, 32:64], SW + " G16", "GS1")
        ext(T.pS, "pS", "SELS", T.GS, "GS0 GS1", True)
        gat("v", T.LD[:, 0:512], T.DG[:], T.L16[:, 0:32], "DG DG0 DG1 L16", "LD0")
        gat("a", T.LD[:, 512:1024], T.DG[:], T.L16[:, 32:64], "DG DG0 DG1 L16", "LD1")
        cp(T.S16[:], T.pS[:, 0:64], "pS", "S16")
        signs(X, xk, T.S16, "S16")
        if n == 0 and k == 0:
            digits("a")
        for c in range(8):
            o = T.pL[:, 8 * c:8 * c + 8]
            mm(o, T.GS[:, 128 * c:128 * c + 128], T.S2P[:], True, False, "GS0 GS1 S2P", "pL")
            mm(o, T.LD[:, 128 * c:128 * c + 128], T.S2N[:], False, True, "LD0 LD1 S2N", "pL")
        clip()
        for c in range(8):
            mm(T.pV[:, 8 * c:8 * c + 8], T.SG[:, 128 * c:128 * c + 128], T.M2[:], True, True,
               "M2 SG%d" % (c >= BS // 8), "pV")
        cp(T.DL[:], T.pL[:, 0:64], "pL", "DL")
        tt(T.D[:], T.pS[:, 0:64], T.L[:], A.subtract, "pS L", "D")
        cp(T.AT[:, 0:512], T.pT0[:, 0:512], "pT0", "AT0")
        if k == 0:
            turned()
        tt(T.SH[:], T.pS[:, 0:64], T.H[:], A.subtract, "pS H", "SH")
        for b in range(NV, 64):
            o, w = 128 * (b % 8) + 16 * (b // 8) + 12, 128 * (b - NV)
            act(T.BT[:, w:w + 128], T.IO[:], F.Abs, "IO AT%d" % (b % 8 // 4), "BT%d" % b, bias=T.AT[:, o:o + 1], scale=-1.0)
        tt(T.AK2[:], T.pV[:, 0:64], T.DL[:], A.is_lt, "pV DL", "AK2")
        act(T.AKN[:], T.AK2[:], F.Copy, "AK2", "AKN", scale=-1.0)
        for b in range(64):
            gr, c = b // 8, b % 8
            o, a = 128 * c + 16 * gr + 12, 8 * c + gr
            bb, ak = T.BB[:, 128 * b:128 * b + 128], T.AK2[:, a:a + 1]
            if b < NV:
                em("v", lambda: g.vector.tensor_scalar(bb, T.IO[:], T.AT[:, o:o + 1], ak, A.is_equal, A.mult),
                   "IO AK2 AT%d" % (c // 4), "BB%d" % b)
            else:
                act(bb, T.BT[:, 128 * (b - NV):128 * (b - NV) + 128], F.Relu, "BT%d AK2 AKN" % b, "BB%d" % b,
                    bias=ak, scale=T.AKN[:, a:a + 1])
        mm(T.pV[:, 0:64], T.I32N[:], T.D[:], True, False, "I32N D", "pV")
        ext(T.pV, "pV", "SELM", T.SG, "SG0 SG1", False)
        for b in range(64):
            gr, c = b // 8, b % 8
            mm(T.pH[:, 16 * gr:16 * gr + 16], T.BB[:, 128 * b:128 * b + 128],
               T.AT[:, 128 * c + 16 * gr:128 * c + 16 * gr + 16], c == 0, c == 7, "BB%d AT%d" % (b, c // 4), "pH")
        ts(T.OI[:], T.H[:], 255, A.bitwise_and, "H", "OI")
        ts(T.N3[:], T.pV[:, 0:64], 0.0, A.is_ge, "pV", "N3", 256.0, A.mult)
        t3("OF", "OI", "N3", A.max)
        cp(T.OF16[:], T.OF[:], "OF", "OF16")
        if n == 0 and k == 0:
            last_constants()
        ts(T.C1[:], T.pH[:, 0:128], 1.0 / 2048, A.mult, "pH", "C1", -0.25, A.add)
        ts(T.C0[:], T.C1[:], 2048.0, A.mult, "C1", "C0", 1.0, A.add)
        ts(T.FL1[:], T.C1[:], 1.0, A.is_equal, "C1", "FL1")
        tt(T.FL0[:], T.pH[:, 0:128], T.C0[:], A.is_equal, "pH C0", "FL0")
        m = 16 * GP
        mm(T.pS[:, 0:1024 - m], T.IDP[:], T.GE[:, m:1024], True, False, "IDP GE1", "pS")
        mm(T.pX[:, 0:64], T.I32P[:], T.TR[:], True, False, "I32P TR", "pX")
        tr(T.pF[:, 128:256], T.FL1[:], "FL1", "pF")
        tr(T.pF[:, 0:128], T.FL0[:], "FL0", "pF")
        cp(T.FT[:, 0:256], T.pF[:, 0:256], "pF", "FT")
        tt(T.GF[:, 0:m], T.FT[:].indirect(T.OF16[:, 0:GP]), T.GE[:, 0:m], A.mult, "FT OF16 GE0 GE1", "GF0")
        gat("a", T.XS[:, 512:1536 - m], T.FT[:], T.OF16[:, GP:64], "FT OF16", "XS1")
        mm(T.pS[:, 0:1024 - m], T.IDF[:], T.XS[:, 512:1536 - m], False, True, "IDF XS1", "pS")
        act(T.GF[:, m:1024], T.pS[:, 0:1024 - m], F.Relu, "pS", "GF1", bias=-4096.0)
        ext(T.pX, "pX", "SELF", T.GF, "GF0 GF1", False)
        if not final:
            t3("WK", "N3", "SIT", A.is_gt)
            ts(T.EL[:], T.D[:], 0.0, A.is_equal, "D", "EL", float(ROOT), A.mult)
            t3("T1", "WK", "SH", A.mult)
            t3("LH", "SH", "D", A.subtract)
            t3("H1", "H", "T1", A.add)
            t3("L1", "L", "EL", A.max)
        if not last:
            ts(T.BI[:], T.LN[:], (ST * n + k + 1) % LB, A.arith_shift_right, "LN", "BI", 1, A.bitwise_and)
            ts(T.AK[:], T.N3[:], 0.0, A.is_equal, "N3", "AK", float(TOP), A.mult)
            t3("AB", "AK", "BI", A.mult)
        tt(T.SC[:], T.pX[:, 0:64], T.H[:], A.max, "pX H", "SC")
        if not final:
            ts(T.SO[:], T.pX[:, 0:64], 0.0, A.is_lt, "pX", "SO")
        cp(T.SC16[:], T.SC[:], "SC", "SC16")
        if not last:
            ts(T.NS[:], T.pX[:, 0:64], 0.0, A.is_ge, "pX", "NS")
        if not final:
            t3("T2", "SO", "LH", A.mult)
            t3("T3", "SO", "D", A.mult)
            if not last:
                t3("SIT", "AB", "NS", A.mult)
            t3("H", "H1", "T2", A.add)
            t3("L", "L1", "T3", A.add)
            if not last:
                t3("G", "H", "SIT", A.max)
                cp(T.L16[:], T.L[:], "L", "L16")
                cp(T.G16[:], T.G[:], "G", "G16")
                digits("a")
                own_x(X, xk)
                turned()
            else:
                ts(T.UP[:], T.L[:], float(ROOT), A.is_equal, "L", "UP")
                tt(T.T1[:], T.EF[:, 0:64], T.H[:], A.subtract, "EF H", "T1")
                tt(T.T2[:], T.EF[:, 64:128], T.L[:], A.subtract, "EF L", "T2")
                t3("SH", "T1", "UP", A.mult)
                t3("D", "T2", "UP", A.mult)
                t3("H1", "SH", "H", A.add)
                t3("T3", "D", "L", A.add)
                sp = "SP%d" % n
                cp(T[sp][:, 0:64], T.H1[:], "H1", "+" + sp)
                cp(T[sp][:, 64:128], T.T3[:], "T3", "+" + sp)
                send(T["LP%d" % n][:], T[sp][:], "r%d" % n, "s%d" % n, sp)
        em("v", lambda: g.vector.tensor_copy(T.SW[:].indirect(T.SC16[:]), T.LD[:]), "SC16 LD0 LD1", SW)
        if last:
            act(T.XP[:], X[:, 0:1536], F.Identity, xk, "XP", bias=1.0)
            act(T.XM[:], X[:, 0:1536], F.Identity, xk, "XM", bias=-1.0)

    def round_end(n, X, xk, Y, yk):
        final = n == RO - 1
        if final:
            dma("s", T.D0[:], T.SW[0:128:16, 0:3072], SW, "D0")
            dma("s", T.D1[:], T.SW[1:128:16, 0:3072], SW, "D1")
        bank = ("pH", "pL", "pX")
        for c in (1, 2, 0):
            mm(T[bank[c]][:], T.IDN[:], X[:, 1536 + 512 * c:2048 + 512 * c], True, False, "IDN " + xk, bank[c])

        def lists(ps, o, key):
            ts(T.R1[:], T[ps][:, 0:64], float(ROOT), A.is_equal, ps, "R1")
            tt(T.R2[:], T.R1[:], T.VM[:, o:o + 64], A.mult, "R1 VM", "R2")
            tt(T.R3[:], T[ps][:, 0:64], T.R2[:], A.add, ps + " R2", "R3")
            cp(T.SL16[:, o:o + 64], T.R3[:], "R3", key)
        ext(T.pS, "pS", "SELS", T.SW, SW, True, 64, 128)
        lists("pS", 128, "SLc")
        ext(T.pV, "pV", "SELS", T.SW, SW, True, 64, 0)
        lists("pV", 0, "SLa")
        ext(T.pS, "pS", "SELS", T.SW, SW, True, 64, 64)
        tt(T.DD[:, 0:1024], X[:].indirect(T.SL16[:, 0:64]), T.XP[:, 0:1024], A.min, xk + " SLa XP", "DDa")
        lists("pS", 64, "SLb")
        mm(T.pV[:], T.IDP[:], T.XM[:, 0:512], True, True, "IDP XM", "pV")
        mm(T.pS[:], T.IDP[:], T.XM[:, 512:1024], True, True, "IDP XM", "pS")

        def ga(c):
            gat("a", T.XS[:, 512 * c:512 * c + 512], X[:], T.SL16[:, 96 + 32 * c:128 + 32 * c],
                xk + (" SLc" if c else " SLb"), "XS%d" % c)
            mm(T[bank[c]][:], T.IDP[:], T.XS[:, 512 * c:512 * c + 512], False, True, "IDP XS%d" % c, bank[c])

        def sg(c):
            act(T.SN[:, 512 * c:512 * c + 512], T[bank[c]][:], F.Sign, bank[c], "SN%d" % c)
            o = 1536 + 512 * c
            mm(T[bank[c]][:], T.IDP[:], X[:, o:o + 512], True, False, "IDP " + xk, bank[c])
            mm(T[bank[c]][:], T.IDP[:], T.SN[:, 512 * c:512 * c + 512], False, True, "IDP SN%d" % c, bank[c])

        def ev(c):
            o = 1536 + 512 * c
            act(Y[:, o:o + 512], T[bank[c]][:], F.Copy, bank[c], "+" + yk + ("b" if c else "d"))
        ga(1), ga(2), sg(1), ga(0), sg(2), ev(1), sg(0), ev(2), ev(0)
        tt(Y[:, 0:512], T.DD[:, 0:512], T.pV[:], A.max, "DDa pV", "+" + yk + "a")
        tt(Y[:, 512:1024], T.DD[:, 512:1024], T.pS[:], A.max, "DDa pS", "+" + yk + "a")
        tt(T.DD[:, 1024:1536], X[:].indirect(T.SL16[:, 64:96]), T.XP[:, 1024:1536], A.min, xk + " SLb XP", "DDb")
        tt(Y[:, 1024:1536], T.DD[:, 1024:1536], T.XM[:, 1024:1536], A.max, "DDb XM", yk + "c")
        if final:
            dma("s", T.yx[:, 0:1024], Y[:, 0:1024], yk + "a", "oxa")
            ts(T.Y2[:], T.D0[:], 64.0, A.mult, "D0", "Y2")
            tt(T.Y3[:], T.Y2[:], T.D1[:], A.add, "Y2 D1", "Y3")
            ts(T.Y2[:], T.Y3[:], float(ROOT), A.is_equal, "Y3", "Y2")
            tt(T.Y2[:], T.Y2[:], T.VK[:], A.mult, "Y2 VK", "Y2")
            tt(T.Y3[:], T.Y3[:], T.Y2[:], A.subtract, "Y3 Y2", "Y3")
            dma("s", T.yx[:, 1024:1536], Y[:, 1024:1536], yk + "c", "oxc")
            dma("s", T.ys[:], T.Y3[:], "Y3", "oy")
            dma("s", T.yx[:, 2048:3072], Y[:, 2048:3072], yk + "b", "oxb")
            dma("s", T.yx[:, 1536:2048], Y[:, 1536:2048], yk + "d", "oxd")

    X, Y, xk, yk = T.XA, T.XB, "X0", "X1"
    for n in range(RO):
        xr = " ".join(xk + c for c in "abcde")
        round_start(n, X, xr)
        for k in range(ST):
            step(n, k, X, xr)
        round_end(n, X, xr, Y, yk)
        X, Y, xk, yk = Y, X, yk, xk
    for s, v in total.items():
        if seen["g"].get(s, 0) < v:
            g.wait_ge(T.sem[s], v)
